import numpy as np
import ml_dtypes


def mxq(x, axis, fmt="e4m3"):
    dtype, down = {"e4m3": (ml_dtypes.float8_e4m3fn, 7), "e5m2": (ml_dtypes.float8_e5m2, 14)}[fmt]
    v = np.moveaxis(np.asarray(x, np.float32).astype(ml_dtypes.bfloat16).astype(np.float64), axis, -1)
    blocks = v.reshape(v.shape[:-1] + (-1, 32))
    amax = np.abs(blocks).max(-1, keepdims=True)
    byte = np.maximum(np.where(amax > 0, np.frexp(amax)[1] - 1 + 127, 0) - down, 1)
    scale = np.exp2(byte - 127.0)
    codes = (blocks / scale).astype(np.float32).astype(dtype).astype(np.float64)
    return np.moveaxis((codes * scale).reshape(v.shape), -1, axis)


WIDE = False


def mx_kscale(k):
    if not WIDE:
        return np.ones(k)
    levels = np.array([10, -10, 5, -5, 0])
    if k % 512:
        return np.exp2(np.random.permutation(np.resize(levels, k // 32))).repeat(32)
    a = np.empty((k // 512, 16))
    for p in range(k // 512):
        a[p, :8] = np.random.permutation(np.resize(levels, 8))
        for g in range(8):
            far = levels[np.abs(levels - a[p, g]) >= 10]
            a[p, g + 8] = far[np.random.randint(len(far))]
    return np.exp2(a.ravel()).repeat(32)


def f64(x):
    return np.asarray(x).astype(np.float64)


def striped(idx):
    return np.tile(np.asarray(idx).reshape(-1, 16).T, (8, 1)).astype(np.uint16)


def unstriped(offs):
    return offs[:16].T.reshape(-1).astype(np.int64)


B, N, T, D, DV, NQ = 1, 512, 2048, 512, 256, 256


def setup_inputs():
    n = np.random.standard_normal
    idx = np.sort(np.random.permutation(T)[:B * N].reshape(B, N), axis=1).reshape(-1)
    s = mx_kscale(D)[:, None]
    u = np.ones(T)
    u[idx] = mx_kscale(B * N)
    r = np.random.uniform(0.5, 2.0, T)
    rk = np.random.uniform(0.5, 2.0, T)
    k = n((D, T)) / s / rk
    v = n((DV, T)) / (u * r)
    return {
        "qT": (n((B, D, NQ)) * s * (0.50 / np.sqrt(D))).astype(np.float32),
        "kT": k.astype(np.float32),
        "vT": v.astype(np.float32),
        "ks": np.tile(rk, (128, 1)).astype(np.float32),
        "vs": np.tile(u * r, (128, 1)).astype(np.float32),
        "og": n((B, NQ, DV)).astype(np.float32),
        "offs": striped(idx),
    }


def reference(qT, kT, vT, ks, vs, og, offs):
    idx = unstriped(offs)
    k = f64(kT)
    v = f64(vT)
    pick = lambda x: x[:, idx].reshape(x.shape[0], B, N).transpose(1, 0, 2)
    q = f64(qT)
    score = mxq(q, 1, "e4m3").transpose(0, 2, 1) @ mxq(pick(k), 1, "e4m3")
    score = score * pick(f64(ks))[:, :1, :]
    m = score.max(-1, keepdims=True)
    p = np.exp(score - m)
    total = p.sum(-1, keepdims=True)
    w = p * pick(f64(vs))[:, :1, :]
    y = mxq(w, 2, "e4m3") @ mxq(pick(v).transpose(0, 2, 1), 1, "e4m3")
    y = y / total
    y = y / (1.0 + np.exp(-f64(og)))
    return y

@@ -1,0 +1,211 @@
+from contextlib import ExitStack
+
+import concourse.mybir as mybir
+from concourse.masks import make_identity
+
+P = 128
+D, NQ, T, N, DV = 512, 256, 2048, 512, 256
+PACK = 4
+S = N // PACK
+
+FLOPS = 2 * NQ * N * D + 2 * NQ * N * DV
+BYTES = 4 * (D * NQ + D * T + DV * T + 2 * T + 2 * NQ * DV) + 2 * P * (N // 16)
+
+F32 = mybir.dt.float32
+BF16 = mybir.dt.bfloat16
+U16 = mybir.dt.uint16
+U32 = mybir.dt.uint32
+U8 = mybir.dt.uint8
+FP8X4 = mybir.dt.float8_e4m3fn_x4
+
+ACT = mybir.ActivationFunctionType
+ALU = mybir.AluOpType
+AX = mybir.AxisListType
+
+
+def tile_attend_gate_topks_kernel(tc, qT, kT, vT, ks, vs, og, offs, out):
+    nc = tc.nc
+    with ExitStack() as ctx:
+        keep = ctx.enter_context(tc.tile_pool(name="keep", bufs=1))
+        psum = ctx.enter_context(tc.psum_pool(name="psum", bufs=2))
+
+        offsets = keep.tile([P, N // 16], U16, name="offsets")
+        scale_win = []
+        for i in range(2):
+            win = keep.tile([P, T], F32, name=f"scale_win{i}")
+            nc.vector.memset(win[:], 0.0)
+            scale_win.append(win)
+
+        k_rows = kT.rearrange("(p t) n -> p t n", t=PACK)
+        k_raw = []
+        for t in range(PACK):
+            plane = keep.tile([P, T], F32, name=f"k_raw{t}")
+            nc.sync.dma_start(out=plane[:], in_=k_rows[:, t, :])
+            k_raw.append(plane)
+            if t == 0:
+                nc.sync.dma_start(offsets[:], offs)
+            if t < 2:
+                nc.sync.dma_start(out=scale_win[t][0:1, :], in_=(ks, vs)[t][0:1, :])
+        q_raw = keep.tile([P, PACK, NQ], F32, name="q_raw")
+        nc.sync.dma_start(out=q_raw[:], in_=qT.rearrange("o (p t) q -> p (o t) q", t=PACK))
+        v_raw = []
+        for e in range(DV // P):
+            block = keep.tile([P, T], F32, name=f"v_raw{e}")
+            nc.sync.dma_start(out=block[:], in_=vT[e * P : (e + 1) * P, :])
+            v_raw.append(block)
+        og_raw = keep.tile([P, 2, DV], F32, name="og_raw")
+        nc.sync.dma_start(out=og_raw[:], in_=og.rearrange("o (b p) e -> p (o b) e", p=P))
+
+        warm = keep.tile([P, 1], F32, name="warm")
+        nc.gpsimd.memset(warm[:], 0.0)
+        warmed = keep.tile([P, 1], F32, name="warmed")
+        nc.scalar.activation(warmed[:], warm[:], ACT.Exp)
+
+        ident = keep.tile([P, P], F32, name="ident")
+        ident_bf = keep.tile([P, P], BF16, name="ident_bf")
+
+        make_identity(nc, ident[:])
+        make_identity(nc, ident_bf[:])
+
+        scale_cols = []
+        for i in range(2):
+            picked = keep.tile([P, N], F32, name=f"scale_row{i}")
+            nc.vector.tensor_copy(picked[:], scale_win[i][:].indirect(offsets[:]))
+            turned = psum.tile([P, PACK, P], F32, tag="a", name=f"scale_turned{i}")
+            for a in range(PACK):
+                nc.tensor.transpose(turned[:, a, :], picked[:, a * S : (a + 1) * S] if i == 0 else picked[:, a::PACK], ident[:])
+            cols = keep.tile([P, PACK], F32, name=f"scale_cols{i}")
+            nc.scalar.copy(cols[:], turned[:, :, 0])
+            scale_cols.append(cols)
+        ks_cols, vs_cols = scale_cols
+
+        k_bf = keep.tile([P, N, PACK], BF16, name="k_bf", align_bytes=64)
+        for t in range(PACK - 1):
+            nc.vector.tensor_copy(k_bf[:, :, t], k_raw[t][:].indirect(offsets[:]))
+        for h in range(2):
+            nc.vector.tensor_copy(
+                k_bf[:, h * 2 * S : (h + 1) * 2 * S, PACK - 1], k_raw[PACK - 1][:].indirect(offsets[:, h * 16 : (h + 1) * 16])
+            )
+        k_codes = keep.tile([P, N], U32, name="k_codes", align_bytes=64)
+        k_scales = keep.tile([P, N], U8, name="k_scales", align_bytes=64)
+        scaled = keep.tile([P, PACK, NQ], F32, name="scaled")
+        for h in range(2):
+            cols = slice(h * 2 * S, (h + 1) * 2 * S)
+            nc.vector.quantize_mx(
+                out=k_codes[:, cols].bitcast(FP8X4),
+                scales=k_scales[:, cols],
+                in_=k_bf[:, cols, :].rearrange("p s t -> p (s t)"),
+            )
+        for b in range(2):
+            queries = slice(b * P, (b + 1) * P)
+            q_bf = keep.tile([P, P, PACK], BF16, name=f"q_bf{b}", align_bytes=64)
+            nc.scalar.copy(q_bf[:], q_raw[:, :, queries].rearrange("p t q -> p q t"))
+            q_codes = keep.tile([P, P], U32, name=f"q_codes{b}", align_bytes=64)
+            q_scales = keep.tile([P, P], U8, name=f"q_scales{b}", align_bytes=64)
+            nc.vector.quantize_mx(out=q_codes[:].bitcast(FP8X4), scales=q_scales[:], in_=q_bf[:].rearrange("p q t -> p (q t)"))
+            scores = psum.tile([P, PACK, P], F32, tag="s", name=f"scores{b}")
+            for a in range(PACK):
+                nc.tensor.matmul_mx(
+                    out=scores[:, a, :],
+                    lhsT=k_codes[:, a * S : (a + 1) * S].bitcast(FP8X4),
+                    lhsT_scale=k_scales[:, a * S : (a + 1) * S],
+                    rhs=q_codes[:].bitcast(FP8X4),
+                    rhs_scale=q_scales[:],
+                    start=True,
+                    stop=True,
+                )
+            for a in range(PACK):
+                if b == 0 and a == 2:
+                    nc.vector.tensor_tensor(scaled[:, 2:, queries], scores[:, 2:, :], ks_cols[:, 2:].unsqueeze(2).to_broadcast([P, 2, P]), ALU.mult)
+                elif b == 1 or a < 2:
+                    nc.scalar.activation(scaled[:, a, queries], scores[:, a, :], ACT.Copy, scale=ks_cols[:, a : a + 1])
+
+        neg_max = []
+        parts = [keep.tile([P, 2], F32, name=f"parts{h}") for h in range(2)]
+        probs = []
+        for b in range(2):
+            rows = psum.tile([P, PACK, S], F32, tag="a", name=f"rows{b}")
+            for a in range(PACK):
+                nc.tensor.transpose(rows[:, a, :], scaled[:, a, b * P : (b + 1) * P], ident[:])
+            top = keep.tile([P, 1], F32, name=f"top{b}")
+            nc.vector.reduce_max(out=top[:], in_=rows[:].rearrange("p a s -> p (a s)"), axis=AX.X, negate=True)
+            prob = keep.tile([P, PACK, S], F32, name=f"prob{b}")
+            by_class = rows[:].rearrange("p n (s a) -> p a n s", a=PACK)
+            for h in range(2):
+                nc.scalar.activation(
+                    prob[:, 2 * h : 2 * h + 2, :].rearrange("p a (n s) -> p a n s", n=PACK),
+                    by_class[:, 2 * h : 2 * h + 2, :, :],
+                    ACT.Exp,
+                    bias=top[:],
+                    accum_out=parts[h][:, b : b + 1],
+                )
+            probs.append(prob)
+
+        sums = keep.tile([P, 2], F32, name="sums")
+        nc.vector.tensor_tensor(sums[:], parts[0][:], parts[1][:], ALU.add)
+        inv = keep.tile([P, 2], F32, name="inv")
+        nc.vector.reciprocal(inv[:], sums[:])
+
+        v_codes, v_scales = [], []
+
+        def pick_values(e):
+            v_bf = keep.tile([P, PACK, S], BF16, name=f"v_bf{e}", align_bytes=64)
+            nc.vector.tensor_copy(v_bf[:].rearrange("p a s -> p s a"), v_raw[e][:].indirect(offsets[:]))
+            turned = psum.tile([P, PACK, P], BF16, tag="v", name=f"v_turned{e}")
+            for a in range(PACK):
+                nc.tensor.transpose(turned[:, a, :], v_bf[:, a, :], ident_bf[:])
+            grouped = keep.tile([P, P, PACK], BF16, name=f"v_grouped{e}", align_bytes=64)
+            nc.scalar.copy(grouped[:], turned[:].rearrange("p a e -> p e a"))
+            codes = keep.tile([P, P], U32, name=f"v_codes{e}", align_bytes=64)
+            scales = keep.tile([P, P], U8, name=f"v_scales{e}", align_bytes=64)
+            nc.vector.quantize_mx(out=codes[:].bitcast(FP8X4), scales=scales[:], in_=grouped[:].rearrange("p e a -> p (e a)"))
+            v_codes.append(codes)
+            v_scales.append(scales)
+
+        pick_values(0)
+
+        gate = keep.tile([P, 2, DV], F32, name="gate")
+        nc.scalar.activation(gate[:], og_raw[:], ACT.Tanh, scale=0.5)
+        factor = keep.tile([P, 2, DV], F32, name="factor")
+
+        w_codes, w_scales = [], []
+        for b in range(2):
+            turned = psum.tile([P, PACK, P], F32, tag="s", name=f"p_turned{b}")
+            for a in range(PACK):
+                nc.tensor.transpose(turned[:, a, :], probs[b][:, a, :], ident[:])
+            w_bf = keep.tile([P, P, PACK], BF16, name=f"w_bf{b}", align_bytes=64)
+            nc.vector.tensor_tensor(
+                w_bf[:],
+                turned[:].rearrange("p a q -> p q a"),
+                vs_cols[:].unsqueeze(1).to_broadcast([P, P, PACK]),
+                ALU.mult,
+            )
+            codes = keep.tile([P, P], U32, name=f"w_codes{b}", align_bytes=64)
+            scales = keep.tile([P, P], U8, name=f"w_scales{b}", align_bytes=64)
+            nc.vector.quantize_mx(out=codes[:].bitcast(FP8X4), scales=scales[:], in_=w_bf[:].rearrange("p q a -> p (q a)"))
+            w_codes.append(codes)
+            w_scales.append(scales)
+
+        pick_values(1)
+
+        for b in range(2):
+            nc.scalar.activation(
+                factor[:, b, :], gate[:, b, :], ACT.Identity, scale=inv[:, b : b + 1], bias=inv[:, b : b + 1]
+            )
+
+        out_rows = out.rearrange("o (b p) e -> p (o b) e", p=P)
+        for e in range(2):
+            y = psum.tile([P, 2, P], F32, tag="y", name=f"y{e}")
+            for b in range(2):
+                nc.tensor.matmul_mx(
+                    out=y[:, b, :],
+                    lhsT=w_codes[b][:].bitcast(FP8X4),
+                    lhsT_scale=w_scales[b][:],
+                    rhs=v_codes[e][:].bitcast(FP8X4),
+                    rhs_scale=v_scales[e][:],
+                    start=True,
+                    stop=True,
+                )
+            result = keep.tile([P, 2, P], F32, name=f"result{e}")
+            nc.vector.scalar_tensor_tensor(result[:], y[:], 0.5, factor[:, :, e * P : (e + 1) * P], ALU.mult, ALU.mult)
+            nc.sync.dma_start(out=out_rows[:, :, e * P : (e + 1) * P], in_=result[:])

@@ -7,6 +7,7 @@ P = 128
 D, NQ, T, N, DV = 512, 256, 2048, 512, 256
 PACK = 4
 S = N // PACK
+RUN = T // P
 
 FLOPS = 2 * NQ * N * D + 2 * NQ * N * DV
 BYTES = 4 * (D * NQ + D * T + DV * T + 2 * T + 2 * NQ * DV) + 2 * P * (N // 16)
@@ -27,14 +28,15 @@ def tile_attend_gate_topks_kernel(tc, qT, kT, vT, ks, vs, og, offs, out):
     nc = tc.nc
     with ExitStack() as ctx:
         keep = ctx.enter_context(tc.tile_pool(name="keep", bufs=1))
-        psum = ctx.enter_context(tc.psum_pool(name="psum", bufs=2))
+        psum = ctx.enter_context(tc.psum_pool(name="psum", bufs=1))
 
         offsets = keep.tile([P, N // 16], U16, name="offsets")
-        scale_win = []
-        for i in range(2):
-            win = keep.tile([P, T], F32, name=f"scale_win{i}")
-            nc.vector.memset(win[:], 0.0)
-            scale_win.append(win)
+        ks_win = keep.tile([P, T], F32, name="ks_win")
+        vs_win = keep.tile([P, T], F32, name="vs_win")
+        nc.vector.memset(vs_win[:], 0.0)
+        scale_win = [ks_win, vs_win]
+        ks_runs = keep.tile([P, RUN], F32, name="ks_runs")
+        nc.sync.dma_start(out=ks_runs[:], in_=ks[0:1, :].rearrange("o (p j) -> (o p) j", j=RUN))
 
         k_rows = kT.rearrange("(p t) n -> p t n", t=PACK)
         k_raw = []
@@ -44,13 +46,13 @@ def tile_attend_gate_topks_kernel(tc, qT, kT, vT, ks, vs, og, offs, out):
             k_raw.append(plane)
             if t == 0:
                 nc.sync.dma_start(offsets[:], offs)
-            if t < 2:
-                nc.sync.dma_start(out=scale_win[t][0:1, :], in_=(ks, vs)[t][0:1, :])
+            if t == 1:
+                nc.sync.dma_start(out=vs_win[0:1, :], in_=vs[0:1, :])
         q_raw = keep.tile([P, PACK, NQ], F32, name="q_raw")
         nc.sync.dma_start(out=q_raw[:], in_=qT.rearrange("o (p t) q -> p (o t) q", t=PACK))
         v_raw = []
         for e in range(DV // P):
-            block = keep.tile([P, T], F32, name=f"v_raw{e}")
+            block = keep.tile([P, T], F32, name=f"v_raw{e}", tag=f"values{e}", align_bytes=64)
             nc.sync.dma_start(out=block[:], in_=vT[e * P : (e + 1) * P, :])
             v_raw.append(block)
         og_raw = keep.tile([P, 2, DV], F32, name="og_raw")
@@ -62,16 +64,24 @@ def tile_attend_gate_topks_kernel(tc, qT, kT, vT, ks, vs, og, offs, out):
         nc.scalar.activation(warmed[:], warm[:], ACT.Exp)
 
         ident = keep.tile([P, P], F32, name="ident")
-        ident_bf = keep.tile([P, P], BF16, name="ident_bf")
 
         make_identity(nc, ident[:])
-        make_identity(nc, ident_bf[:])
+
+        for g in range(RUN // PACK):
+            spread = psum.tile([P, PACK, P], F32, tag=f"bank{g}", name=f"spread{g}")
+            for j in range(PACK):
+                col = PACK * g + j
+                nc.tensor.transpose(spread[:, j, :], ks_runs[:, col : col + 1].to_broadcast([P, P]), ident[:])
+            nc.scalar.copy(
+                ks_win[:].rearrange("m (p j) -> m p j", j=RUN)[:, :, PACK * g : PACK * (g + 1)],
+                spread[:].rearrange("m j p -> m p j"),
+            )
 
         scale_cols = []
         for i in range(2):
             picked = keep.tile([P, N], F32, name=f"scale_row{i}")
             nc.vector.tensor_copy(picked[:], scale_win[i][:].indirect(offsets[:]))
-            turned = psum.tile([P, PACK, P], F32, tag="a", name=f"scale_turned{i}")
+            turned = psum.tile([P, PACK, P], F32, tag=f"bank{6 + i}", name=f"scale_turned{i}")
             for a in range(PACK):
                 nc.tensor.transpose(turned[:, a, :], picked[:, a * S : (a + 1) * S] if i == 0 else picked[:, a::PACK], ident[:])
             cols = keep.tile([P, PACK], F32, name=f"scale_cols{i}")
@@ -86,49 +96,70 @@ def tile_attend_gate_topks_kernel(tc, qT, kT, vT, ks, vs, og, offs, out):
             nc.vector.tensor_copy(
                 k_bf[:, h * 2 * S : (h + 1) * 2 * S, PACK - 1], k_raw[PACK - 1][:].indirect(offsets[:, h * 16 : (h + 1) * 16])
             )
-        k_codes = keep.tile([P, N], U32, name="k_codes", align_bytes=64)
-        k_scales = keep.tile([P, N], U8, name="k_scales", align_bytes=64)
-        scaled = keep.tile([P, PACK, NQ], F32, name="scaled")
-        for h in range(2):
-            cols = slice(h * 2 * S, (h + 1) * 2 * S)
-            nc.vector.quantize_mx(
-                out=k_codes[:, cols].bitcast(FP8X4),
-                scales=k_scales[:, cols],
-                in_=k_bf[:, cols, :].rearrange("p s t -> p (s t)"),
+        q_bf = []
+        for b in range(2):
+            grouped = keep.tile([P, P, PACK], BF16, name=f"q_bf{b}", tag=f"q_bf{b}", align_bytes=64)
+            nc.scalar.copy(grouped[:], q_raw[:, :, b * P : (b + 1) * P].rearrange("p t q -> p q t"))
+            q_bf.append(grouped)
+
+        def quantise(name, source, width, tag):
+            codes = keep.tile([P, width], U32, name=f"{name}_codes", tag=tag, align_bytes=64)
+            scales = keep.tile([P, width], U8, name=f"{name}_scales", align_bytes=64)
+            nc.vector.quantize_mx(out=codes[:].bitcast(FP8X4), scales=scales[:], in_=source)
+            return codes, scales
+
+        k_mx, q_mx = [], []
+        for i in range(2):
+            k_mx.append(
+                quantise(f"k{i}", k_bf[:, i * 2 * S : (i + 1) * 2 * S, :].rearrange("p s t -> p (s t)"), 2 * S, f"k{i}")
             )
+            q_mx.append(quantise(f"q{i}", q_bf[i][:].rearrange("p q t -> p (q t)"), P, f"q{i}"))
+
+        scaled = keep.tile([P, PACK, NQ], F32, name="scaled")
         for b in range(2):
             queries = slice(b * P, (b + 1) * P)
-            q_bf = keep.tile([P, P, PACK], BF16, name=f"q_bf{b}", align_bytes=64)
-            nc.scalar.copy(q_bf[:], q_raw[:, :, queries].rearrange("p t q -> p q t"))
-            q_codes = keep.tile([P, P], U32, name=f"q_codes{b}", align_bytes=64)
-            q_scales = keep.tile([P, P], U8, name=f"q_scales{b}", align_bytes=64)
-            nc.vector.quantize_mx(out=q_codes[:].bitcast(FP8X4), scales=q_scales[:], in_=q_bf[:].rearrange("p q t -> p (q t)"))
-            scores = psum.tile([P, PACK, P], F32, tag="s", name=f"scores{b}")
-            for a in range(PACK):
-                nc.tensor.matmul_mx(
-                    out=scores[:, a, :],
-                    lhsT=k_codes[:, a * S : (a + 1) * S].bitcast(FP8X4),
-                    lhsT_scale=k_scales[:, a * S : (a + 1) * S],
-                    rhs=q_codes[:].bitcast(FP8X4),
-                    rhs_scale=q_scales[:],
-                    start=True,
-                    stop=True,
-                )
-            for a in range(PACK):
-                if b == 0 and a == 2:
-                    nc.vector.tensor_tensor(scaled[:, 2:, queries], scores[:, 2:, :], ks_cols[:, 2:].unsqueeze(2).to_broadcast([P, 2, P]), ALU.mult)
-                elif b == 1 or a < 2:
-                    nc.scalar.activation(scaled[:, a, queries], scores[:, a, :], ACT.Copy, scale=ks_cols[:, a : a + 1])
+            for h in range(2):
+                scores = psum.tile([P, 2, P], F32, tag=f"bank{2 * b + h}", name=f"scores{b}{h}")
+                for j in range(2):
+                    nc.tensor.matmul_mx(
+                        out=scores[:, j, :],
+                        lhsT=k_mx[h][0][:, j * S : (j + 1) * S].bitcast(FP8X4),
+                        lhsT_scale=k_mx[h][1][:, j * S : (j + 1) * S],
+                        rhs=q_mx[b][0][:].bitcast(FP8X4),
+                        rhs_scale=q_mx[b][1][:],
+                        start=True,
+                        stop=True,
+                    )
+                for j in range(2):
+                    a = 2 * h + j
+                    nc.scalar.activation(scaled[:, a, queries], scores[:, j, :], ACT.Copy, scale=ks_cols[:, a : a + 1])
+
+        v_words = []
+        for e in range(DV // P):
+            v_bf = keep.tile([P, 2, S, 2], BF16, name=f"v_bf{e}", tag=("q_bf1", "v_bf1")[e], align_bytes=64)
+            nc.vector.tensor_copy(v_bf[:].rearrange("f u p t -> f p u t"), v_raw[e][:].indirect(offsets[:]))
+            v_words.append(v_bf[:].rearrange("f u p t -> f (u p t)").bitcast(F32))
+        v_grouped = keep.tile([P, DV * PACK], BF16, name="v_grouped", align_bytes=64)
+
+        def turn_values(e):
+            turned = psum.tile([P, 2, P], F32, tag=f"bank{3 + 2 * e}", name=f"v_turned{e}")
+            for u in range(2):
+                nc.tensor.transpose(turned[:, u, :], v_words[e][:, u * S : (u + 1) * S], ident[:])
+            nc.scalar.copy(
+                v_grouped[:].bitcast(F32).rearrange("p (f u) -> p f u", u=2)[:, e * P : (e + 1) * P, :],
+                turned[:].rearrange("p u f -> p f u"),
+            )
 
         neg_max = []
         parts = [keep.tile([P, 2], F32, name=f"parts{h}") for h in range(2)]
         probs = []
         for b in range(2):
-            rows = psum.tile([P, PACK, S], F32, tag="a", name=f"rows{b}")
+            rows = psum.tile([P, PACK, S], F32, tag=f"bank{4 + b}", name=f"rows{b}")
             for a in range(PACK):
                 nc.tensor.transpose(rows[:, a, :], scaled[:, a, b * P : (b + 1) * P], ident[:])
-            top = keep.tile([P, 1], F32, name=f"top{b}")
+            top = keep.tile([P, 1], F32, name=f"top{b}", tag=("values0", "top1")[b], align_bytes=64)
             nc.vector.reduce_max(out=top[:], in_=rows[:].rearrange("p a s -> p (a s)"), axis=AX.X, negate=True)
+            neg_max.append(top)
             prob = keep.tile([P, PACK, S], F32, name=f"prob{b}")
             by_class = rows[:].rearrange("p n (s a) -> p a n s", a=PACK)
             for h in range(2):
@@ -146,66 +177,47 @@ def tile_attend_gate_topks_kernel(tc, qT, kT, vT, ks, vs, og, offs, out):
         inv = keep.tile([P, 2], F32, name="inv")
         nc.vector.reciprocal(inv[:], sums[:])
 
-        v_codes, v_scales = [], []
-
-        def pick_values(e):
-            v_bf = keep.tile([P, PACK, S], BF16, name=f"v_bf{e}", align_bytes=64)
-            nc.vector.tensor_copy(v_bf[:].rearrange("p a s -> p s a"), v_raw[e][:].indirect(offsets[:]))
-            turned = psum.tile([P, PACK, P], BF16, tag="v", name=f"v_turned{e}")
-            for a in range(PACK):
-                nc.tensor.transpose(turned[:, a, :], v_bf[:, a, :], ident_bf[:])
-            grouped = keep.tile([P, P, PACK], BF16, name=f"v_grouped{e}", align_bytes=64)
-            nc.scalar.copy(grouped[:], turned[:].rearrange("p a e -> p e a"))
-            codes = keep.tile([P, P], U32, name=f"v_codes{e}", align_bytes=64)
-            scales = keep.tile([P, P], U8, name=f"v_scales{e}", align_bytes=64)
-            nc.vector.quantize_mx(out=codes[:].bitcast(FP8X4), scales=scales[:], in_=grouped[:].rearrange("p e a -> p (e a)"))
-            v_codes.append(codes)
-            v_scales.append(scales)
-
-        pick_values(0)
-
-        gate = keep.tile([P, 2, DV], F32, name="gate")
-        nc.scalar.activation(gate[:], og_raw[:], ACT.Tanh, scale=0.5)
-        factor = keep.tile([P, 2, DV], F32, name="factor")
-
-        w_codes, w_scales = [], []
+        turn_values(0)
+        p_turned = []
         for b in range(2):
-            turned = psum.tile([P, PACK, P], F32, tag="s", name=f"p_turned{b}")
+            turned = psum.tile([P, PACK, P], F32, tag=f"bank{6 + b}", name=f"p_turned{b}")
             for a in range(PACK):
                 nc.tensor.transpose(turned[:, a, :], probs[b][:, a, :], ident[:])
-            w_bf = keep.tile([P, P, PACK], BF16, name=f"w_bf{b}", align_bytes=64)
+            p_turned.append(turned)
+        turn_values(1)
+
+        half = keep.tile([P, 2, DV], F32, name="half")
+        nc.scalar.activation(half[:], og_raw[:], ACT.Tanh, scale=0.5)
+        gate = keep.tile([P, 2, DV], F32, name="gate")
+        nc.scalar.activation(gate[:], half[:], ACT.Identity, scale=0.5, bias=0.5)
+
+        w_bf = []
+        for b in range(2):
+            weights = keep.tile([P, P, PACK], BF16, name=f"w_bf{b}", tag=("values1", "w_bf1")[b], align_bytes=64)
             nc.vector.tensor_tensor(
-                w_bf[:],
-                turned[:].rearrange("p a q -> p q a"),
+                weights[:],
+                p_turned[b][:].rearrange("p a q -> p q a"),
                 vs_cols[:].unsqueeze(1).to_broadcast([P, P, PACK]),
                 ALU.mult,
             )
-            codes = keep.tile([P, P], U32, name=f"w_codes{b}", align_bytes=64)
-            scales = keep.tile([P, P], U8, name=f"w_scales{b}", align_bytes=64)
-            nc.vector.quantize_mx(out=codes[:].bitcast(FP8X4), scales=scales[:], in_=w_bf[:].rearrange("p q a -> p (q a)"))
-            w_codes.append(codes)
-            w_scales.append(scales)
-
-        pick_values(1)
-
+            w_bf.append(weights)
+        v_codes = keep.tile([P, DV], U32, name="v_codes", align_bytes=64)
+        v_scales = keep.tile([P, DV], U8, name="v_scales", align_bytes=64)
+        nc.vector.quantize_mx(out=v_codes[:].bitcast(FP8X4), scales=v_scales[:], in_=v_grouped[:])
         for b in range(2):
-            nc.scalar.activation(
-                factor[:, b, :], gate[:, b, :], ACT.Identity, scale=inv[:, b : b + 1], bias=inv[:, b : b + 1]
+            w_codes = keep.tile([P, P], U32, name=f"w_codes{b}", align_bytes=64)
+            w_scales = keep.tile([P, P], U8, name=f"w_scales{b}", align_bytes=64)
+            nc.vector.quantize_mx(out=w_codes[:].bitcast(FP8X4), scales=w_scales[:], in_=w_bf[b][:].rearrange("p q a -> p (q a)"))
+            y = psum.tile([P, DV], F32, tag=f"bank{b}", name=f"y{b}")
+            nc.tensor.matmul_mx(
+                out=y[:],
+                lhsT=w_codes[:].bitcast(FP8X4),
+                lhsT_scale=w_scales[:],
+                rhs=v_codes[:].bitcast(FP8X4),
+                rhs_scale=v_scales[:],
+                start=True,
+                stop=True,
             )
-
-        out_rows = out.rearrange("o (b p) e -> p (o b) e", p=P)
-        for e in range(2):
-            y = psum.tile([P, 2, P], F32, tag="y", name=f"y{e}")
-            for b in range(2):
-                nc.tensor.matmul_mx(
-                    out=y[:, b, :],
-                    lhsT=w_codes[b][:].bitcast(FP8X4),
-                    lhsT_scale=w_scales[b][:],
-                    rhs=v_codes[e][:].bitcast(FP8X4),
-                    rhs_scale=v_scales[e][:],
-                    start=True,
-                    stop=True,
-                )
-            result = keep.tile([P, 2, P], F32, name=f"result{e}")
-            nc.vector.scalar_tensor_tensor(result[:], y[:], 0.5, factor[:, :, e * P : (e + 1) * P], ALU.mult, ALU.mult)
-            nc.sync.dma_start(out=out_rows[:, :, e * P : (e + 1) * P], in_=result[:])
+            result = keep.tile([P, DV], F32, name=f"result{b}")
+            nc.vector.scalar_tensor_tensor(result[:], y[:], inv[:, b : b + 1], gate[:, b, :], ALU.mult, ALU.mult)
+            nc.sync.dma_start(out=out[0, b * P : (b + 1) * P, :], in_=result[:])

@@ -32,7 +32,7 @@ def tile_attend_gate_topks_kernel(tc, qT, kT, vT, ks, vs, og, offs, out):
 
         offsets = keep.tile([P, N // 16], U16, name="offsets")
         ks_win = keep.tile([P, T], F32, name="ks_win")
-        vs_win = keep.tile([P, T], F32, name="vs_win")
+        vs_win = keep.tile([P, T], F32, name="vs_win", tag="vs_win", align_bytes=64)
         nc.vector.memset(vs_win[:], 0.0)
         scale_win = [ks_win, vs_win]
         ks_runs = keep.tile([P, RUN], F32, name="ks_runs")
@@ -41,12 +41,11 @@ def tile_attend_gate_topks_kernel(tc, qT, kT, vT, ks, vs, og, offs, out):
         k_rows = kT.rearrange("(p t) n -> p t n", t=PACK)
         k_raw = []
         for t in range(PACK):
-            plane = keep.tile([P, T], F32, name=f"k_raw{t}")
+            plane = keep.tile([P, T], F32, name=f"k_raw{t}", tag=f"k_raw{t}")
             nc.sync.dma_start(out=plane[:], in_=k_rows[:, t, :])
             k_raw.append(plane)
             if t == 0:
                 nc.sync.dma_start(offsets[:], offs)
-            if t == 1:
                 nc.sync.dma_start(out=vs_win[0:1, :], in_=vs[0:1, :])
         q_raw = keep.tile([P, PACK, NQ], F32, name="q_raw")
         nc.sync.dma_start(out=q_raw[:], in_=qT.rearrange("o (p t) q -> p (o t) q", t=PACK))
@@ -77,9 +76,16 @@ def tile_attend_gate_topks_kernel(tc, qT, kT, vT, ks, vs, og, offs, out):
                 spread[:].rearrange("m j p -> m p j"),
             )
 
+        k_bf = keep.tile([P, N, PACK], BF16, name="k_bf", align_bytes=64)
+        for t in range(PACK - 1):
+            nc.vector.tensor_copy(k_bf[:, :, t], k_raw[t][:].indirect(offsets[:]))
+        for h in range(2):
+            nc.vector.tensor_copy(
+                k_bf[:, h * 2 * S : (h + 1) * 2 * S, PACK - 1], k_raw[PACK - 1][:].indirect(offsets[:, h * 16 : (h + 1) * 16])
+            )
         scale_cols = []
         for i in range(2):
-            picked = keep.tile([P, N], F32, name=f"scale_row{i}")
+            picked = keep.tile([P, N], F32, name=f"scale_row{i}", tag=("k_raw1", "scale_row1")[i])
             nc.vector.tensor_copy(picked[:], scale_win[i][:].indirect(offsets[:]))
             turned = psum.tile([P, PACK, P], F32, tag=f"bank{6 + i}", name=f"scale_turned{i}")
             for a in range(PACK):
@@ -89,13 +95,6 @@ def tile_attend_gate_topks_kernel(tc, qT, kT, vT, ks, vs, og, offs, out):
             scale_cols.append(cols)
         ks_cols, vs_cols = scale_cols
 
-        k_bf = keep.tile([P, N, PACK], BF16, name="k_bf", align_bytes=64)
-        for t in range(PACK - 1):
-            nc.vector.tensor_copy(k_bf[:, :, t], k_raw[t][:].indirect(offsets[:]))
-        for h in range(2):
-            nc.vector.tensor_copy(
-                k_bf[:, h * 2 * S : (h + 1) * 2 * S, PACK - 1], k_raw[PACK - 1][:].indirect(offsets[:, h * 16 : (h + 1) * 16])
-            )
         q_bf = []
         for b in range(2):
             grouped = keep.tile([P, P, PACK], BF16, name=f"q_bf{b}", tag=f"q_bf{b}", align_bytes=64)
@@ -136,19 +135,18 @@ def tile_attend_gate_topks_kernel(tc, qT, kT, vT, ks, vs, og, offs, out):
 
         v_words = []
         for e in range(DV // P):
-            v_bf = keep.tile([P, 2, S, 2], BF16, name=f"v_bf{e}", tag=("q_bf1", "v_bf1")[e], align_bytes=64)
-            nc.vector.tensor_copy(v_bf[:].rearrange("f u p t -> f p u t"), v_raw[e][:].indirect(offsets[:]))
-            v_words.append(v_bf[:].rearrange("f u p t -> f (u p t)").bitcast(F32))
-        v_grouped = keep.tile([P, DV * PACK], BF16, name="v_grouped", align_bytes=64)
+            v_bf = keep.tile([P, N], BF16, name=f"v_bf{e}", align_bytes=64)
+            nc.vector.tensor_copy(v_bf[:], v_raw[e][:].indirect(offsets[:]))
+            v_words.append(v_bf[:].bitcast(F32))
+        v_grouped = []
 
         def turn_values(e):
             turned = psum.tile([P, 2, P], F32, tag=f"bank{3 + 2 * e}", name=f"v_turned{e}")
             for u in range(2):
-                nc.tensor.transpose(turned[:, u, :], v_words[e][:, u * S : (u + 1) * S], ident[:])
-            nc.scalar.copy(
-                v_grouped[:].bitcast(F32).rearrange("p (f u) -> p f u", u=2)[:, e * P : (e + 1) * P, :],
-                turned[:].rearrange("p u f -> p f u"),
-            )
+                nc.tensor.transpose(turned[:, u, :], v_words[e][:, u::2], ident[:])
+            grouped = keep.tile([P, P * PACK], BF16, name=f"v_grouped{e}", tag=("top1", "v_grouped1")[e], align_bytes=64)
+            nc.scalar.copy(grouped[:].bitcast(F32).rearrange("p (f u) -> p f u", u=2), turned[:].rearrange("p u f -> p f u"))
+            v_grouped.append(grouped)
 
         neg_max = []
         parts = [keep.tile([P, 2], F32, name=f"parts{h}") for h in range(2)]
@@ -157,7 +155,7 @@ def tile_attend_gate_topks_kernel(tc, qT, kT, vT, ks, vs, og, offs, out):
             rows = psum.tile([P, PACK, S], F32, tag=f"bank{4 + b}", name=f"rows{b}")
             for a in range(PACK):
                 nc.tensor.transpose(rows[:, a, :], scaled[:, a, b * P : (b + 1) * P], ident[:])
-            top = keep.tile([P, 1], F32, name=f"top{b}", tag=("values0", "top1")[b], align_bytes=64)
+            top = keep.tile([P, 1], F32, name=f"top{b}", tag=f"top{b}", align_bytes=64)
             nc.vector.reduce_max(out=top[:], in_=rows[:].rearrange("p a s -> p (a s)"), axis=AX.X, negate=True)
             neg_max.append(top)
             prob = keep.tile([P, PACK, S], F32, name=f"prob{b}")
@@ -191,9 +189,11 @@ def tile_attend_gate_topks_kernel(tc, qT, kT, vT, ks, vs, og, offs, out):
         gate = keep.tile([P, 2, DV], F32, name="gate")
         nc.scalar.activation(gate[:], half[:], ACT.Identity, scale=0.5, bias=0.5)
 
+        v_codes = keep.tile([P, DV], U32, name="v_codes", align_bytes=64)
+        v_scales = keep.tile([P, DV], U8, name="v_scales", align_bytes=64)
         w_bf = []
         for b in range(2):
-            weights = keep.tile([P, P, PACK], BF16, name=f"w_bf{b}", tag=("values1", "w_bf1")[b], align_bytes=64)
+            weights = keep.tile([P, P, PACK], BF16, name=f"w_bf{b}", align_bytes=64)
             nc.vector.tensor_tensor(
                 weights[:],
                 p_turned[b][:].rearrange("p a q -> p q a"),
@@ -201,13 +201,10 @@ def tile_attend_gate_topks_kernel(tc, qT, kT, vT, ks, vs, og, offs, out):
                 ALU.mult,
             )
             w_bf.append(weights)
-        v_codes = keep.tile([P, DV], U32, name="v_codes", align_bytes=64)
-        v_scales = keep.tile([P, DV], U8, name="v_scales", align_bytes=64)
-        nc.vector.quantize_mx(out=v_codes[:].bitcast(FP8X4), scales=v_scales[:], in_=v_grouped[:])
+            cols = slice(b * P, (b + 1) * P)
+            nc.vector.quantize_mx(out=v_codes[:, cols].bitcast(FP8X4), scales=v_scales[:, cols], in_=v_grouped[b][:])
         for b in range(2):
-            w_codes = keep.tile([P, P], U32, name=f"w_codes{b}", align_bytes=64)
-            w_scales = keep.tile([P, P], U8, name=f"w_scales{b}", align_bytes=64)
-            nc.vector.quantize_mx(out=w_codes[:].bitcast(FP8X4), scales=w_scales[:], in_=w_bf[b][:].rearrange("p q a -> p (q a)"))
+            w_codes, w_scales = quantise(f"w{b}", w_bf[b][:].rearrange("p q a -> p (q a)"), P, ("w0", "v_grouped1")[b])
             y = psum.tile([P, DV], F32, tag=f"bank{b}", name=f"y{b}")
             nc.tensor.matmul_mx(
                 out=y[:],

@@ -46,6 +46,7 @@ def tile_attend_gate_topks_kernel(tc, qT, kT, vT, ks, vs, og, offs, out):
             k_raw.append(plane)
             if t == 0:
                 nc.sync.dma_start(offsets[:], offs)
+            if t == 1:
                 nc.sync.dma_start(out=vs_win[0:1, :], in_=vs[0:1, :])
         q_raw = keep.tile([P, PACK, NQ], F32, name="q_raw")
         nc.sync.dma_start(out=q_raw[:], in_=qT.rearrange("o (p t) q -> p (o t) q", t=PACK))
@@ -76,16 +77,13 @@ def tile_attend_gate_topks_kernel(tc, qT, kT, vT, ks, vs, og, offs, out):
                 spread[:].rearrange("m j p -> m p j"),
             )
 
-        k_bf = keep.tile([P, N, PACK], BF16, name="k_bf", align_bytes=64)
-        for t in range(PACK - 1):
-            nc.vector.tensor_copy(k_bf[:, :, t], k_raw[t][:].indirect(offsets[:]))
-        for h in range(2):
-            nc.vector.tensor_copy(
-                k_bf[:, h * 2 * S : (h + 1) * 2 * S, PACK - 1], k_raw[PACK - 1][:].indirect(offsets[:, h * 16 : (h + 1) * 16])
-            )
+        k_bf = [keep.tile([P, 2 * S, PACK], BF16, name=f"k_half{h}", align_bytes=64) for h in range(2)]
+        for t in range(PACK):
+            for h in range(2):
+                nc.vector.tensor_copy(k_bf[h][:, :, t], k_raw[t][:].indirect(offsets[:, h * 16 : (h + 1) * 16]))
         scale_cols = []
         for i in range(2):
-            picked = keep.tile([P, N], F32, name=f"scale_row{i}", tag=("k_raw1", "scale_row1")[i])
+            picked = keep.tile([P, N], F32, name=f"scale_row{i}")
             nc.vector.tensor_copy(picked[:], scale_win[i][:].indirect(offsets[:]))
             turned = psum.tile([P, PACK, P], F32, tag=f"bank{6 + i}", name=f"scale_turned{i}")
             for a in range(PACK):
@@ -98,7 +96,10 @@ def tile_attend_gate_topks_kernel(tc, qT, kT, vT, ks, vs, og, offs, out):
         q_bf = []
         for b in range(2):
             grouped = keep.tile([P, P, PACK], BF16, name=f"q_bf{b}", tag=f"q_bf{b}", align_bytes=64)
-            nc.scalar.copy(grouped[:], q_raw[:, :, b * P : (b + 1) * P].rearrange("p t q -> p q t"))
+            nc.scalar.copy(
+                grouped[:].rearrange("p (c i) t -> p c t i", i=PACK),
+                q_raw[:, :, b * P : (b + 1) * P].rearrange("p t (c i) -> p c t i", i=PACK),
+            )
             q_bf.append(grouped)
 
         def quantise(name, source, width, tag):
@@ -110,7 +111,7 @@ def tile_attend_gate_topks_kernel(tc, qT, kT, vT, ks, vs, og, offs, out):
         k_mx, q_mx = [], []
         for i in range(2):
             k_mx.append(
-                quantise(f"k{i}", k_bf[:, i * 2 * S : (i + 1) * 2 * S, :].rearrange("p s t -> p (s t)"), 2 * S, f"k{i}")
+                quantise(f"k{i}", k_bf[i][:].rearrange("p s t -> p (s t)"), 2 * S, f"k{i}")
             )
             q_mx.append(quantise(f"q{i}", q_bf[i][:].rearrange("p q t -> p (q t)"), P, f"q{i}"))
 
@@ -135,7 +136,7 @@ def tile_attend_gate_topks_kernel(tc, qT, kT, vT, ks, vs, og, offs, out):
 
         v_words = []
         for e in range(DV // P):
-            v_bf = keep.tile([P, N], BF16, name=f"v_bf{e}", align_bytes=64)
+            v_bf = keep.tile([P, N], BF16, name=f"v_bf{e}", tag=f"v_bf{e}", align_bytes=64)
             nc.vector.tensor_copy(v_bf[:], v_raw[e][:].indirect(offsets[:]))
             v_words.append(v_bf[:].bitcast(F32))
         v_grouped = []
@@ -186,14 +187,14 @@ def tile_attend_gate_topks_kernel(tc, qT, kT, vT, ks, vs, og, offs, out):
 
         half = keep.tile([P, 2, DV], F32, name="half")
         nc.scalar.activation(half[:], og_raw[:], ACT.Tanh, scale=0.5)
-        gate = keep.tile([P, 2, DV], F32, name="gate")
+        gate = keep.tile([P, 2, DV], F32, name="gate", tag="v_bf1", align_bytes=64)
         nc.scalar.activation(gate[:], half[:], ACT.Identity, scale=0.5, bias=0.5)
 
         v_codes = keep.tile([P, DV], U32, name="v_codes", align_bytes=64)
         v_scales = keep.tile([P, DV], U8, name="v_scales", align_bytes=64)
         w_bf = []
         for b in range(2):
-            weights = keep.tile([P, P, PACK], BF16, name=f"w_bf{b}", align_bytes=64)
+            weights = keep.tile([P, P, PACK], BF16, name=f"w_bf{b}", tag=("values1", "w_bf1")[b], align_bytes=64)
             nc.vector.tensor_tensor(
                 weights[:],
                 p_turned[b][:].rearrange("p a q -> p q a"),

@@ -7,7 +7,6 @@ P = 128
 D, NQ, T, N, DV = 512, 256, 2048, 512, 256
 PACK = 4
 S = N // PACK
-RUN = T // P
 
 FLOPS = 2 * NQ * N * D + 2 * NQ * N * DV
 BYTES = 4 * (D * NQ + D * T + DV * T + 2 * T + 2 * NQ * DV) + 2 * P * (N // 16)
@@ -28,15 +27,15 @@ def tile_attend_gate_topks_kernel(tc, qT, kT, vT, ks, vs, og, offs, out):
     nc = tc.nc
     with ExitStack() as ctx:
         keep = ctx.enter_context(tc.tile_pool(name="keep", bufs=1))
+        late = ctx.enter_context(tc.tile_pool(name="late", bufs=1))
         psum = ctx.enter_context(tc.psum_pool(name="psum", bufs=1))
 
         offsets = keep.tile([P, N // 16], U16, name="offsets")
         ks_win = keep.tile([P, T], F32, name="ks_win")
         vs_win = keep.tile([P, T], F32, name="vs_win", tag="vs_win", align_bytes=64)
+        nc.vector.memset(ks_win[:], 0.0)
         nc.vector.memset(vs_win[:], 0.0)
         scale_win = [ks_win, vs_win]
-        ks_runs = keep.tile([P, RUN], F32, name="ks_runs")
-        nc.sync.dma_start(out=ks_runs[:], in_=ks[0:1, :].rearrange("o (p j) -> (o p) j", j=RUN))
 
         k_rows = kT.rearrange("(p t) n -> p t n", t=PACK)
         k_raw = []
@@ -46,13 +45,13 @@ def tile_attend_gate_topks_kernel(tc, qT, kT, vT, ks, vs, og, offs, out):
             k_raw.append(plane)
             if t == 0:
                 nc.sync.dma_start(offsets[:], offs)
-            if t == 1:
-                nc.sync.dma_start(out=vs_win[0:1, :], in_=vs[0:1, :])
+            if t < 2:
+                nc.sync.dma_start(out=scale_win[t][64 * t : 64 * t + 1, :], in_=(ks, vs)[t][0:1, :])
         q_raw = keep.tile([P, PACK, NQ], F32, name="q_raw")
         nc.sync.dma_start(out=q_raw[:], in_=qT.rearrange("o (p t) q -> p (o t) q", t=PACK))
         v_raw = []
         for e in range(DV // P):
-            block = keep.tile([P, T], F32, name=f"v_raw{e}", tag=f"values{e}", align_bytes=64)
+            block = late.tile([P, T], F32, name=f"v_raw{e}", align_bytes=64, offset=e * 4 * T)
             nc.sync.dma_start(out=block[:], in_=vT[e * P : (e + 1) * P, :])
             v_raw.append(block)
         og_raw = keep.tile([P, 2, DV], F32, name="og_raw")
@@ -67,16 +66,6 @@ def tile_attend_gate_topks_kernel(tc, qT, kT, vT, ks, vs, og, offs, out):
 
         make_identity(nc, ident[:])
 
-        for g in range(RUN // PACK):
-            spread = psum.tile([P, PACK, P], F32, tag=f"bank{g}", name=f"spread{g}")
-            for j in range(PACK):
-                col = PACK * g + j
-                nc.tensor.transpose(spread[:, j, :], ks_runs[:, col : col + 1].to_broadcast([P, P]), ident[:])
-            nc.scalar.copy(
-                ks_win[:].rearrange("m (p j) -> m p j", j=RUN)[:, :, PACK * g : PACK * (g + 1)],
-                spread[:].rearrange("m j p -> m p j"),
-            )
-
         k_bf = [keep.tile([P, 2 * S, PACK], BF16, name=f"k_half{h}", align_bytes=64) for h in range(2)]
         for t in range(PACK):
             for h in range(2):
@@ -89,7 +78,7 @@ def tile_attend_gate_topks_kernel(tc, qT, kT, vT, ks, vs, og, offs, out):
             for a in range(PACK):
                 nc.tensor.transpose(turned[:, a, :], picked[:, a * S : (a + 1) * S] if i == 0 else picked[:, a::PACK], ident[:])
             cols = keep.tile([P, PACK], F32, name=f"scale_cols{i}")
-            nc.scalar.copy(cols[:], turned[:, :, 0])
+            nc.scalar.copy(cols[:], turned[:, :, 64 * i])
             scale_cols.append(cols)
         ks_cols, vs_cols = scale_cols
 
@@ -171,11 +160,6 @@ def tile_attend_gate_topks_kernel(tc, qT, kT, vT, ks, vs, og, offs, out):
                 )
             probs.append(prob)
 
-        sums = keep.tile([P, 2], F32, name="sums")
-        nc.vector.tensor_tensor(sums[:], parts[0][:], parts[1][:], ALU.add)
-        inv = keep.tile([P, 2], F32, name="inv")
-        nc.vector.reciprocal(inv[:], sums[:])
-
         turn_values(0)
         p_turned = []
         for b in range(2):
@@ -190,11 +174,11 @@ def tile_attend_gate_topks_kernel(tc, qT, kT, vT, ks, vs, og, offs, out):
         gate = keep.tile([P, 2, DV], F32, name="gate", tag="v_bf1", align_bytes=64)
         nc.scalar.activation(gate[:], half[:], ACT.Identity, scale=0.5, bias=0.5)
 
-        v_codes = keep.tile([P, DV], U32, name="v_codes", align_bytes=64)
+        v_codes = late.tile([P, DV], U32, name="v_codes", align_bytes=64, offset=4 * T + 2048)
         v_scales = keep.tile([P, DV], U8, name="v_scales", align_bytes=64)
         w_bf = []
         for b in range(2):
-            weights = keep.tile([P, P, PACK], BF16, name=f"w_bf{b}", tag=("values1", "w_bf1")[b], align_bytes=64)
+            weights = late.tile([P, P, PACK], BF16, name=f"w_bf{b}", align_bytes=64, offset=4 * T + 1024 * b)
             nc.vector.tensor_tensor(
                 weights[:],
                 p_turned[b][:].rearrange("p a q -> p q a"),
@@ -202,10 +186,18 @@ def tile_attend_gate_topks_kernel(tc, qT, kT, vT, ks, vs, og, offs, out):
                 ALU.mult,
             )
             w_bf.append(weights)
-            cols = slice(b * P, (b + 1) * P)
-            nc.vector.quantize_mx(out=v_codes[:, cols].bitcast(FP8X4), scales=v_scales[:, cols], in_=v_grouped[b][:])
+        w_mx = [quantise("w0", w_bf[0][:].rearrange("p q a -> p (q a)"), P, "w0")]
+        for e in range(2):
+            cols = slice(e * P, (e + 1) * P)
+            nc.vector.quantize_mx(out=v_codes[:, cols].bitcast(FP8X4), scales=v_scales[:, cols], in_=v_grouped[e][:])
+        w_mx.append(quantise("w1", w_bf[1][:].rearrange("p q a -> p (q a)"), P, "w1"))
+        sums = late.tile([P, 2], F32, name="sums", align_bytes=64, offset=4 * T + 3072)
+        nc.vector.tensor_tensor(sums[:], parts[0][:], parts[1][:], ALU.add)
+        inv = keep.tile([P, 2], F32, name="inv")
+        nc.vector.reciprocal(inv[:], sums[:])
+
         for b in range(2):
-            w_codes, w_scales = quantise(f"w{b}", w_bf[b][:].rearrange("p q a -> p (q a)"), P, ("w0", "v_grouped1")[b])
+            w_codes, w_scales = w_mx[b]
             y = psum.tile([P, DV], F32, tag=f"bank{b}", name=f"y{b}")
             nc.tensor.matmul_mx(
                 out=y[:],

@@ -7,6 +7,7 @@ P = 128
 D, NQ, T, N, DV = 512, 256, 2048, 512, 256
 PACK = 4
 S = N // PACK
+LEAD = 3 * T // 4
 
 FLOPS = 2 * NQ * N * D + 2 * NQ * N * DV
 BYTES = 4 * (D * NQ + D * T + DV * T + 2 * T + 2 * NQ * DV) + 2 * P * (N // 16)
@@ -41,12 +42,16 @@ def tile_attend_gate_topks_kernel(tc, qT, kT, vT, ks, vs, og, offs, out):
         k_raw = []
         for t in range(PACK):
             plane = keep.tile([P, T], F32, name=f"k_raw{t}", tag=f"k_raw{t}")
-            nc.sync.dma_start(out=plane[:], in_=k_rows[:, t, :])
-            k_raw.append(plane)
             if t == 0:
+                nc.sync.dma_start(out=plane[:, :LEAD], in_=k_rows[:, t, :LEAD])
                 nc.sync.dma_start(offsets[:], offs)
-            if t < 2:
-                nc.sync.dma_start(out=scale_win[t][64 * t : 64 * t + 1, :], in_=(ks, vs)[t][0:1, :])
+                nc.sync.dma_start(out=ks_win[0:1, :], in_=ks[0:1, :])
+                nc.sync.dma_start(out=plane[:, LEAD:], in_=k_rows[:, t, LEAD:])
+            else:
+                nc.sync.dma_start(out=plane[:], in_=k_rows[:, t, :])
+            if t == 1:
+                nc.sync.dma_start(out=vs_win[64:65, :], in_=vs[0:1, :])
+            k_raw.append(plane)
         q_raw = keep.tile([P, PACK, NQ], F32, name="q_raw")
         nc.sync.dma_start(out=q_raw[:], in_=qT.rearrange("o (p t) q -> p (o t) q", t=PACK))
         v_raw = []

@@ -139,7 +139,7 @@ def tile_attend_gate_topks_kernel(tc, qT, kT, vT, ks, vs, og, offs, out):
             turned = psum.tile([P, 2, P], F32, tag=f"bank{3 + 2 * e}", name=f"v_turned{e}")
             for u in range(2):
                 nc.tensor.transpose(turned[:, u, :], v_words[e][:, u::2], ident[:])
-            grouped = keep.tile([P, P * PACK], BF16, name=f"v_grouped{e}", tag=("top1", "v_grouped1")[e], align_bytes=64)
+            grouped = keep.tile([P, P * PACK], BF16, name=f"v_grouped{e}", tag=("top0", "v_grouped1")[e], align_bytes=64)
             nc.scalar.copy(grouped[:].bitcast(F32).rearrange("p (f u) -> p f u", u=2), turned[:].rearrange("p u f -> p f u"))
             v_grouped.append(grouped)
 
@@ -177,25 +177,30 @@ def tile_attend_gate_topks_kernel(tc, qT, kT, vT, ks, vs, og, offs, out):
         half = keep.tile([P, 2, DV], F32, name="half")
         nc.scalar.activation(half[:], og_raw[:], ACT.Tanh, scale=0.5)
         gate = keep.tile([P, 2, DV], F32, name="gate", tag="v_bf1", align_bytes=64)
-        nc.scalar.activation(gate[:], half[:], ACT.Identity, scale=0.5, bias=0.5)
+        for b in range(2):
+            nc.scalar.activation(gate[:, b, :], half[:, b, :], ACT.Identity, scale=0.5, bias=0.5)
 
         v_codes = late.tile([P, DV], U32, name="v_codes", align_bytes=64, offset=4 * T + 2048)
         v_scales = keep.tile([P, DV], U8, name="v_scales", align_bytes=64)
-        w_bf = []
-        for b in range(2):
-            weights = late.tile([P, P, PACK], BF16, name=f"w_bf{b}", align_bytes=64, offset=4 * T + 1024 * b)
+        def weigh(b, weights):
             nc.vector.tensor_tensor(
                 weights[:],
                 p_turned[b][:].rearrange("p a q -> p q a"),
                 vs_cols[:].unsqueeze(1).to_broadcast([P, P, PACK]),
                 ALU.mult,
             )
-            w_bf.append(weights)
-        w_mx = [quantise("w0", w_bf[0][:].rearrange("p q a -> p (q a)"), P, "w0")]
-        for e in range(2):
+            return weights[:].rearrange("p q a -> p (q a)")
+
+        def quantise_values(e):
             cols = slice(e * P, (e + 1) * P)
             nc.vector.quantize_mx(out=v_codes[:, cols].bitcast(FP8X4), scales=v_scales[:, cols], in_=v_grouped[e][:])
-        w_mx.append(quantise("w1", w_bf[1][:].rearrange("p q a -> p (q a)"), P, "w1"))
+
+        w_first = weigh(0, keep.tile([P, P, PACK], BF16, name="w_bf0", tag="top1", align_bytes=64))
+        quantise_values(0)
+        w_second = weigh(1, late.tile([P, P, PACK], BF16, name="w_bf1", align_bytes=64, offset=4 * T))
+        w_mx = [quantise("w0", w_first, P, "w0")]
+        quantise_values(1)
+        w_mx.append(quantise("w1", w_second, P, "w1"))
         sums = late.tile([P, 2], F32, name="sums", align_bytes=64, offset=4 * T + 3072)
         nc.vector.tensor_tensor(sums[:], parts[0][:], parts[1][:], ALU.add)
         inv = keep.tile([P, 2], F32, name="inv")
@@ -204,15 +209,17 @@ def tile_attend_gate_topks_kernel(tc, qT, kT, vT, ks, vs, og, offs, out):
         for b in range(2):
             w_codes, w_scales = w_mx[b]
             y = psum.tile([P, DV], F32, tag=f"bank{b}", name=f"y{b}")
-            nc.tensor.matmul_mx(
-                out=y[:],
-                lhsT=w_codes[:].bitcast(FP8X4),
-                lhsT_scale=w_scales[:],
-                rhs=v_codes[:].bitcast(FP8X4),
-                rhs_scale=v_scales[:],
-                start=True,
-                stop=True,
-            )
+            for e in range(2):
+                cols = slice(e * P, (e + 1) * P)
+                nc.tensor.matmul_mx(
+                    out=y[:, cols],
+                    lhsT=w_codes[:].bitcast(FP8X4),
+                    lhsT_scale=w_scales[:],
+                    rhs=v_codes[:, cols].bitcast(FP8X4),
+                    rhs_scale=v_scales[:, cols],
+                    start=True,
+                    stop=True,
+                )
             result = keep.tile([P, DV], F32, name=f"result{b}")
             nc.vector.scalar_tensor_tensor(result[:], y[:], inv[:, b : b + 1], gate[:, b, :], ALU.mult, ALU.mult)
             nc.sync.dma_start(out=out[0, b * P : (b + 1) * P, :], in_=result[:])

@@ -62,12 +62,12 @@ def tile_attend_gate_topks_kernel(tc, qT, kT, vT, ks, vs, og, offs, out):
         og_raw = keep.tile([P, 2, DV], F32, name="og_raw")
         nc.sync.dma_start(out=og_raw[:], in_=og.rearrange("o (b p) e -> p (o b) e", p=P))
 
-        warm = keep.tile([P, 1], F32, name="warm")
+        warm = keep.tile([P, 1], F32, name="warm", tag="ident")
         nc.gpsimd.memset(warm[:], 0.0)
         warmed = keep.tile([P, 1], F32, name="warmed")
         nc.scalar.activation(warmed[:], warm[:], ACT.Exp)
 
-        ident = keep.tile([P, P], F32, name="ident")
+        ident = keep.tile([P, P], F32, name="ident", tag="ident")
 
         make_identity(nc, ident[:])
 

@@ -8,6 +8,7 @@ D, NQ, T, N, DV = 512, 256, 2048, 512, 256
 PACK = 4
 S = N // PACK
 LEAD = 3 * T // 4
+HEAD = T - N // 2
 
 FLOPS = 2 * NQ * N * D + 2 * NQ * N * DV
 BYTES = 4 * (D * NQ + D * T + DV * T + 2 * T + 2 * NQ * DV) + 2 * P * (N // 16)
@@ -57,18 +58,16 @@ def tile_attend_gate_topks_kernel(tc, qT, kT, vT, ks, vs, og, offs, out):
         v_raw = []
         for e in range(DV // P):
             block = late.tile([P, T], F32, name=f"v_raw{e}", align_bytes=64, offset=e * 4 * T)
-            nc.sync.dma_start(out=block[:], in_=vT[e * P : (e + 1) * P, :])
+            if e == 0:
+                nc.sync.dma_start(out=block[:, :HEAD], in_=vT[:P, :HEAD])
+                nc.sync.dma_start(out=block[:, HEAD:], in_=vT[:P, HEAD:])
+            else:
+                nc.sync.dma_start(out=block[:], in_=vT[e * P : (e + 1) * P, :])
             v_raw.append(block)
         og_raw = keep.tile([P, 2, DV], F32, name="og_raw")
         nc.sync.dma_start(out=og_raw[:], in_=og.rearrange("o (b p) e -> p (o b) e", p=P))
 
-        warm = keep.tile([P, 1], F32, name="warm", tag="ident")
-        nc.gpsimd.memset(warm[:], 0.0)
-        warmed = keep.tile([P, 1], F32, name="warmed")
-        nc.scalar.activation(warmed[:], warm[:], ACT.Exp)
-
-        ident = keep.tile([P, P], F32, name="ident", tag="ident")
-
+        ident = keep.tile([P, P], F32, name="ident")
         make_identity(nc, ident[:])
 
         k_bf = [keep.tile([P, 2 * S, PACK], BF16, name=f"k_half{h}", align_bytes=64) for h in range(2)]
@@ -131,15 +130,23 @@ def tile_attend_gate_topks_kernel(tc, qT, kT, vT, ks, vs, og, offs, out):
         v_words = []
         for e in range(DV // P):
             v_bf = keep.tile([P, N], BF16, name=f"v_bf{e}", tag=f"v_bf{e}", align_bytes=64)
-            nc.vector.tensor_copy(v_bf[:], v_raw[e][:].indirect(offsets[:]))
+            if e == 0:
+                dealt = v_bf[:].rearrange("p (u s i) -> p s u i", u=2, i=2)
+                nc.vector.tensor_copy(dealt[:, : S // 2], v_raw[e][:, :HEAD].indirect(offsets[:, :16]))
+                nc.vector.tensor_copy(dealt[:, S // 2 :], v_raw[e][:].indirect(offsets[:, 16:]))
+            else:
+                nc.vector.tensor_copy(v_bf[:], v_raw[e][:].indirect(offsets[:]))
             v_words.append(v_bf[:].bitcast(F32))
         v_grouped = []
 
         def turn_values(e):
             turned = psum.tile([P, 2, P], F32, tag=f"bank{3 + 2 * e}", name=f"v_turned{e}")
             for u in range(2):
-                nc.tensor.transpose(turned[:, u, :], v_words[e][:, u::2], ident[:])
-            grouped = keep.tile([P, P * PACK], BF16, name=f"v_grouped{e}", tag=("top0", "v_grouped1")[e], align_bytes=64)
+                nc.tensor.transpose(turned[:, u, :], v_words[e][:, u::2] if e == 1 else v_words[e][:, u * S : (u + 1) * S], ident[:])
+            if e == 0:
+                grouped = late.tile([P, P * PACK], BF16, name="v_grouped0", align_bytes=64, offset=0)
+            else:
+                grouped = keep.tile([P, P * PACK], BF16, name="v_grouped1", align_bytes=64)
             nc.scalar.copy(grouped[:].bitcast(F32).rearrange("p (f u) -> p f u", u=2), turned[:].rearrange("p u f -> p f u"))
             v_grouped.append(grouped)
 
@@ -150,7 +157,10 @@ def tile_attend_gate_topks_kernel(tc, qT, kT, vT, ks, vs, og, offs, out):
             rows = psum.tile([P, PACK, S], F32, tag=f"bank{4 + b}", name=f"rows{b}")
             for a in range(PACK):
                 nc.tensor.transpose(rows[:, a, :], scaled[:, a, b * P : (b + 1) * P], ident[:])
-            top = keep.tile([P, 1], F32, name=f"top{b}", tag=f"top{b}", align_bytes=64)
+            if b == 0:
+                top = late.tile([P, 1], F32, name="top0", align_bytes=64, offset=0)
+            else:
+                top = late.tile([P, 1], F32, name="top1", align_bytes=64, offset=2048)
             nc.vector.reduce_max(out=top[:], in_=rows[:].rearrange("p a s -> p (a s)"), axis=AX.X, negate=True)
             neg_max.append(top)
             prob = keep.tile([P, PACK, S], F32, name=f"prob{b}")
@@ -195,7 +205,7 @@ def tile_attend_gate_topks_kernel(tc, qT, kT, vT, ks, vs, og, offs, out):
             cols = slice(e * P, (e + 1) * P)
             nc.vector.quantize_mx(out=v_codes[:, cols].bitcast(FP8X4), scales=v_scales[:, cols], in_=v_grouped[e][:])
 
-        w_first = weigh(0, keep.tile([P, P, PACK], BF16, name="w_bf0", tag="top1", align_bytes=64))
+        w_first = weigh(0, late.tile([P, P, PACK], BF16, name="w_bf0", align_bytes=64, offset=4 * T + 4096))
         quantise_values(0)
         w_second = weigh(1, late.tile([P, P, PACK], BF16, name="w_bf1", align_bytes=64, offset=4 * T))
         w_mx = [quantise("w0", w_first, P, "w0")]

@@ -48,6 +48,8 @@ def tile_attend_gate_topks_kernel(tc, qT, kT, vT, ks, vs, og, offs, out):
                 nc.sync.dma_start(offsets[:], offs)
                 nc.sync.dma_start(out=ks_win[0:1, :], in_=ks[0:1, :])
                 nc.sync.dma_start(out=plane[:, LEAD:], in_=k_rows[:, t, LEAD:])
+            elif t == PACK - 1:
+                nc.sync.dma_start(out=plane[:, :HEAD], in_=k_rows[:, t, :HEAD])
             else:
                 nc.sync.dma_start(out=plane[:], in_=k_rows[:, t, :])
             if t == 1:
@@ -55,6 +57,7 @@ def tile_attend_gate_topks_kernel(tc, qT, kT, vT, ks, vs, og, offs, out):
             k_raw.append(plane)
         q_raw = keep.tile([P, PACK, NQ], F32, name="q_raw")
         nc.sync.dma_start(out=q_raw[:], in_=qT.rearrange("o (p t) q -> p (o t) q", t=PACK))
+        nc.sync.dma_start(out=k_raw[PACK - 1][:, HEAD:], in_=k_rows[:, PACK - 1, HEAD:])
         v_raw = []
         for e in range(DV // P):
             block = late.tile([P, T], F32, name=f"v_raw{e}", align_bytes=64, offset=e * 4 * T)
@@ -73,7 +76,7 @@ def tile_attend_gate_topks_kernel(tc, qT, kT, vT, ks, vs, og, offs, out):
         k_bf = [keep.tile([P, 2 * S, PACK], BF16, name=f"k_half{h}", align_bytes=64) for h in range(2)]
         for t in range(PACK):
             for h in range(2):
-                nc.vector.tensor_copy(k_bf[h][:, :, t], k_raw[t][:].indirect(offsets[:, h * 16 : (h + 1) * 16]))
+                nc.vector.tensor_copy(k_bf[h][:, :, t], k_raw[t][:, : HEAD if h == 0 else T].indirect(offsets[:, h * 16 : (h + 1) * 16]))
         scale_cols = []
         for i in range(2):
             picked = keep.tile([P, N], F32, name=f"scale_row{i}")

@@ -208,7 +208,7 @@ def tile_attend_gate_topks_kernel(tc, qT, kT, vT, ks, vs, og, offs, out):
             cols = slice(e * P, (e + 1) * P)
             nc.vector.quantize_mx(out=v_codes[:, cols].bitcast(FP8X4), scales=v_scales[:, cols], in_=v_grouped[e][:])
 
-        w_first = weigh(0, late.tile([P, P, PACK], BF16, name="w_bf0", align_bytes=64, offset=4 * T + 4096))
+        w_first = weigh(0, late.tile([P, P, PACK], BF16, name="w_bf0", align_bytes=64, offset=2048))
         quantise_values(0)
         w_second = weigh(1, late.tile([P, P, PACK], BF16, name="w_bf1", align_bytes=64, offset=4 * T))
         w_mx = [quantise("w0", w_first, P, "w0")]

@@ -208,24 +208,24 @@ def tile_attend_gate_topks_kernel(tc, qT, kT, vT, ks, vs, og, offs, out):
             cols = slice(e * P, (e + 1) * P)
             nc.vector.quantize_mx(out=v_codes[:, cols].bitcast(FP8X4), scales=v_scales[:, cols], in_=v_grouped[e][:])
 
+        sums = keep.tile([P, 2], F32, name="sums")
+        nc.gpsimd.tensor_tensor(sums[:], parts[0][:], parts[1][:], ALU.add)
         w_first = weigh(0, late.tile([P, P, PACK], BF16, name="w_bf0", align_bytes=64, offset=2048))
+        inv = late.tile([P, 2], F32, name="inv", align_bytes=64, offset=4 * T + 3072)
+        nc.vector.reciprocal(inv[:], sums[:])
         quantise_values(0)
         w_second = weigh(1, late.tile([P, P, PACK], BF16, name="w_bf1", align_bytes=64, offset=4 * T))
-        w_mx = [quantise("w0", w_first, P, "w0")]
+        w_mx = [quantise("w0", w_first, P, "w0"), quantise("w1", w_second, P, "w1")]
         quantise_values(1)
-        w_mx.append(quantise("w1", w_second, P, "w1"))
-        sums = late.tile([P, 2], F32, name="sums", align_bytes=64, offset=4 * T + 3072)
-        nc.vector.tensor_tensor(sums[:], parts[0][:], parts[1][:], ALU.add)
-        inv = keep.tile([P, 2], F32, name="inv")
-        nc.vector.reciprocal(inv[:], sums[:])
 
-        for b in range(2):
-            w_codes, w_scales = w_mx[b]
-            y = psum.tile([P, DV], F32, tag=f"bank{b}", name=f"y{b}")
-            for e in range(2):
-                cols = slice(e * P, (e + 1) * P)
+        result = [keep.tile([P, DV], F32, name=f"result{b}") for b in range(2)]
+        for e in range(2):
+            cols = slice(e * P, (e + 1) * P)
+            for b in range(2):
+                w_codes, w_scales = w_mx[b]
+                y = psum.tile([P, P], F32, tag=f"bank{2 * e + b}", name=f"y{b}{e}")
                 nc.tensor.matmul_mx(
-                    out=y[:, cols],
+                    out=y[:],
                     lhsT=w_codes[:].bitcast(FP8X4),
                     lhsT_scale=w_scales[:],
                     rhs=v_codes[:, cols].bitcast(FP8X4),
@@ -233,6 +233,6 @@ def tile_attend_gate_topks_kernel(tc, qT, kT, vT, ks, vs, og, offs, out):
                     start=True,
                     stop=True,
                 )
-            result = keep.tile([P, DV], F32, name=f"result{b}")
-            nc.vector.scalar_tensor_tensor(result[:], y[:], inv[:, b : b + 1], gate[:, b, :], ALU.mult, ALU.mult)
-            nc.sync.dma_start(out=out[0, b * P : (b + 1) * P, :], in_=result[:])
+                nc.vector.scalar_tensor_tensor(result[b][:, cols], y[:], inv[:, b : b + 1], gate[:, b, cols], ALU.mult, ALU.mult)
+                if e == 1:
+                    nc.sync.dma_start(out=out[0, b * P : (b + 1) * P, :], in_=result[b][:])

@@ -106,29 +106,32 @@ def tile_attend_gate_topks_kernel(tc, qT, kT, vT, ks, vs, og, offs, out):
 
         k_mx, q_mx = [], []
         for i in range(2):
-            k_mx.append(
-                quantise(f"k{i}", k_bf[i][:].rearrange("p s t -> p (s t)"), 2 * S, f"k{i}")
-            )
+            if i == 0:
+                codes, scales = quantise("k0", k_bf[0][:].rearrange("p s t -> p (s t)"), 2 * S, "k0")
+                k_mx.extend((codes[:, j * S : (j + 1) * S], scales[:, j * S : (j + 1) * S]) for j in range(2))
+            else:
+                for j in range(2):
+                    codes, scales = quantise(f"k1{j}", k_bf[1][:, j * S : (j + 1) * S, :].rearrange("p s t -> p (s t)"), S, f"k1{j}")
+                    k_mx.append((codes[:], scales[:]))
             q_mx.append(quantise(f"q{i}", q_bf[i][:].rearrange("p q t -> p (q t)"), P, f"q{i}"))
 
         scaled = keep.tile([P, PACK, NQ], F32, name="scaled")
         for b in range(2):
             queries = slice(b * P, (b + 1) * P)
             for h in range(2):
-                scores = psum.tile([P, 2, P], F32, tag=f"bank{2 * b + h}", name=f"scores{b}{h}")
                 for j in range(2):
+                    scores = psum.tile([P, P], F32, tag=f"bank{(4 * b + 2 * h + j + 4) % 8}", name=f"scores{b}{h}{j}")
                     nc.tensor.matmul_mx(
-                        out=scores[:, j, :],
-                        lhsT=k_mx[h][0][:, j * S : (j + 1) * S].bitcast(FP8X4),
-                        lhsT_scale=k_mx[h][1][:, j * S : (j + 1) * S],
+                        out=scores[:],
+                        lhsT=k_mx[2 * h + j][0].bitcast(FP8X4),
+                        lhsT_scale=k_mx[2 * h + j][1],
                         rhs=q_mx[b][0][:].bitcast(FP8X4),
                         rhs_scale=q_mx[b][1][:],
                         start=True,
                         stop=True,
                     )
-                for j in range(2):
                     a = 2 * h + j
-                    nc.scalar.activation(scaled[:, a, queries], scores[:, j, :], ACT.Copy, scale=ks_cols[:, a : a + 1])
+                    nc.scalar.activation(scaled[:, a, queries], scores[:], ACT.Copy, scale=ks_cols[:, a : a + 1])
 
         v_words = []
         for e in range(DV // P):

@@ -7,8 +7,10 @@ P = 128
 D, NQ, T, N, DV = 512, 256, 2048, 512, 256
 PACK = 4
 S = N // PACK
-LEAD = 3 * T // 4
-HEAD = T - N // 2
+HALF = N // 2
+HEAD = T - HALF
+ROW = P - 1
+SHARE = 3 * N // 4
 
 FLOPS = 2 * NQ * N * D + 2 * NQ * N * DV
 BYTES = 4 * (D * NQ + D * T + DV * T + 2 * T + 2 * NQ * DV) + 2 * P * (N // 16)
@@ -33,39 +35,26 @@ def tile_attend_gate_topks_kernel(tc, qT, kT, vT, ks, vs, og, offs, out):
         psum = ctx.enter_context(tc.psum_pool(name="psum", bufs=1))
 
         offsets = keep.tile([P, N // 16], U16, name="offsets")
-        ks_win = keep.tile([P, T], F32, name="ks_win")
-        vs_win = keep.tile([P, T], F32, name="vs_win", tag="vs_win", align_bytes=64)
-        nc.vector.memset(ks_win[:], 0.0)
-        nc.vector.memset(vs_win[:], 0.0)
-        scale_win = [ks_win, vs_win]
+        scale_win = [keep.tile([P, T], F32, name=f"scale_win{i}") for i in range(2)]
+        for win in scale_win:
+            nc.vector.memset(win[:ROW, :], 0.0)
 
         k_rows = kT.rearrange("(p t) n -> p t n", t=PACK)
-        k_raw = []
-        for t in range(PACK):
-            plane = keep.tile([P, T], F32, name=f"k_raw{t}", tag=f"k_raw{t}")
-            if t == 0:
-                nc.sync.dma_start(out=plane[:, :LEAD], in_=k_rows[:, t, :LEAD])
-                nc.sync.dma_start(offsets[:], offs)
-                nc.sync.dma_start(out=ks_win[0:1, :], in_=ks[0:1, :])
-                nc.sync.dma_start(out=plane[:, LEAD:], in_=k_rows[:, t, LEAD:])
-            elif t == PACK - 1:
-                nc.sync.dma_start(out=plane[:, :HEAD], in_=k_rows[:, t, :HEAD])
-            else:
-                nc.sync.dma_start(out=plane[:], in_=k_rows[:, t, :])
-            if t == 1:
-                nc.sync.dma_start(out=vs_win[64:65, :], in_=vs[0:1, :])
-            k_raw.append(plane)
+        k_raw = [keep.tile([P, T], F32, name=f"k_raw{t}") for t in range(PACK)]
+        nc.sync.dma_start(out=k_raw[0][:], in_=k_rows[:, 0, :])
+        nc.sync.dma_start(offsets[:], offs)
+        nc.sync.dma_start(out=scale_win[0][ROW:, :], in_=ks[0:1, :])
+        nc.sync.dma_start(out=scale_win[1][ROW:, :], in_=vs[0:1, :])
+        nc.sync.dma_start(out=k_raw[1][:], in_=k_rows[:, 1, :])
+        nc.sync.dma_start(out=k_raw[2][:], in_=k_rows[:, 2, :])
+        nc.sync.dma_start(out=k_raw[3][:, :HEAD], in_=k_rows[:, 3, :HEAD])
         q_raw = keep.tile([P, PACK, NQ], F32, name="q_raw")
         nc.sync.dma_start(out=q_raw[:], in_=qT.rearrange("o (p t) q -> p (o t) q", t=PACK))
-        nc.sync.dma_start(out=k_raw[PACK - 1][:, HEAD:], in_=k_rows[:, PACK - 1, HEAD:])
+        nc.sync.dma_start(out=k_raw[3][:, HEAD:], in_=k_rows[:, 3, HEAD:])
         v_raw = []
         for e in range(DV // P):
             block = late.tile([P, T], F32, name=f"v_raw{e}", align_bytes=64, offset=e * 4 * T)
-            if e == 0:
-                nc.sync.dma_start(out=block[:, :HEAD], in_=vT[:P, :HEAD])
-                nc.sync.dma_start(out=block[:, HEAD:], in_=vT[:P, HEAD:])
-            else:
-                nc.sync.dma_start(out=block[:], in_=vT[e * P : (e + 1) * P, :])
+            nc.sync.dma_start(out=block[:], in_=vT[e * P : (e + 1) * P, :])
             v_raw.append(block)
         og_raw = keep.tile([P, 2, DV], F32, name="og_raw")
         nc.sync.dma_start(out=og_raw[:], in_=og.rearrange("o (b p) e -> p (o b) e", p=P))
@@ -73,115 +62,103 @@ def tile_attend_gate_topks_kernel(tc, qT, kT, vT, ks, vs, og, offs, out):
         ident = keep.tile([P, P], F32, name="ident")
         make_identity(nc, ident[:])
 
-        k_bf = [keep.tile([P, 2 * S, PACK], BF16, name=f"k_half{h}", align_bytes=64) for h in range(2)]
+        k_bf = [keep.tile([P, HALF, PACK], BF16, name=f"k_half{h}", align_bytes=64) for h in range(2)]
         for t in range(PACK):
             for h in range(2):
                 nc.vector.tensor_copy(k_bf[h][:, :, t], k_raw[t][:, : HEAD if h == 0 else T].indirect(offsets[:, h * 16 : (h + 1) * 16]))
+
         scale_cols = []
         for i in range(2):
-            picked = keep.tile([P, N], F32, name=f"scale_row{i}")
-            nc.vector.tensor_copy(picked[:], scale_win[i][:].indirect(offsets[:]))
-            turned = psum.tile([P, PACK, P], F32, tag=f"bank{6 + i}", name=f"scale_turned{i}")
+            picked = keep.tile([P, N], F32, name=f"scale_row{i}", tag="scale_row")
+            if i == 0:
+                nc.vector.tensor_copy(picked[:], scale_win[i][:].indirect(offsets[:]))
+            else:
+                nc.scalar.activation(picked[:], scale_win[i][:].indirect(offsets[:]), ACT.Copy)
+            turned = psum.tile([P, PACK, P], F32, tag=f"bank{i}", name=f"scale_turned{i}")
             for a in range(PACK):
-                nc.tensor.transpose(turned[:, a, :], picked[:, a * S : (a + 1) * S] if i == 0 else picked[:, a::PACK], ident[:])
+                nc.tensor.transpose(turned[:, a, :], picked[:, a::PACK], ident[:])
             cols = keep.tile([P, PACK], F32, name=f"scale_cols{i}")
-            nc.scalar.copy(cols[:], turned[:, :, 64 * i])
+            nc.scalar.copy(cols[:], turned[:, :, ROW])
             scale_cols.append(cols)
         ks_cols, vs_cols = scale_cols
+        spread = psum.tile([P, PACK, S], F32, tag="bank2", name="ks_spread")
+        for a in range(PACK):
+            nc.tensor.transpose(spread[:, a, :], ks_cols[:, a : a + 1].to_broadcast([P, P]), ident[:])
+        ks_row = keep.tile([P, PACK, S], F32, name="ks_row")
+        nc.scalar.copy(ks_row[:], spread[:])
 
         q_bf = []
         for b in range(2):
-            grouped = keep.tile([P, P, PACK], BF16, name=f"q_bf{b}", tag=f"q_bf{b}", align_bytes=64)
+            grouped = keep.tile([P, P, PACK], BF16, name=f"q_bf{b}", align_bytes=64)
             nc.scalar.copy(
                 grouped[:].rearrange("p (c i) t -> p c t i", i=PACK),
                 q_raw[:, :, b * P : (b + 1) * P].rearrange("p t (c i) -> p c t i", i=PACK),
             )
             q_bf.append(grouped)
 
-        def quantise(name, source, width, tag):
-            codes = keep.tile([P, width], U32, name=f"{name}_codes", tag=tag, align_bytes=64)
+        def quantise(name, source, width, offset=None):
+            if offset is None:
+                codes = keep.tile([P, width], U32, name=f"{name}_codes", align_bytes=64)
+            else:
+                codes = late.tile([P, width], U32, name=f"{name}_codes", align_bytes=64, offset=offset)
             scales = keep.tile([P, width], U8, name=f"{name}_scales", align_bytes=64)
             nc.vector.quantize_mx(out=codes[:].bitcast(FP8X4), scales=scales[:], in_=source)
             return codes, scales
 
         k_mx, q_mx = [], []
         for i in range(2):
-            if i == 0:
-                codes, scales = quantise("k0", k_bf[0][:].rearrange("p s t -> p (s t)"), 2 * S, "k0")
-                k_mx.extend((codes[:, j * S : (j + 1) * S], scales[:, j * S : (j + 1) * S]) for j in range(2))
-            else:
-                for j in range(2):
-                    codes, scales = quantise(f"k1{j}", k_bf[1][:, j * S : (j + 1) * S, :].rearrange("p s t -> p (s t)"), S, f"k1{j}")
-                    k_mx.append((codes[:], scales[:]))
-            q_mx.append(quantise(f"q{i}", q_bf[i][:].rearrange("p q t -> p (q t)"), P, f"q{i}"))
+            k_mx.append(quantise(f"k{i}", k_bf[i][:].rearrange("p s t -> p (s t)"), HALF))
+            q_mx.append(quantise(f"q{i}", q_bf[i][:].rearrange("p q t -> p (q t)"), P))
 
-        scaled = keep.tile([P, PACK, NQ], F32, name="scaled")
+        scaled = [keep.tile([P, PACK, S], F32, name=f"scaled{b}") for b in range(2)]
         for b in range(2):
-            queries = slice(b * P, (b + 1) * P)
             for h in range(2):
-                for j in range(2):
-                    scores = psum.tile([P, P], F32, tag=f"bank{(4 * b + 2 * h + j + 4) % 8}", name=f"scores{b}{h}{j}")
-                    nc.tensor.matmul_mx(
-                        out=scores[:],
-                        lhsT=k_mx[2 * h + j][0].bitcast(FP8X4),
-                        lhsT_scale=k_mx[2 * h + j][1],
-                        rhs=q_mx[b][0][:].bitcast(FP8X4),
-                        rhs_scale=q_mx[b][1][:],
-                        start=True,
-                        stop=True,
-                    )
-                    a = 2 * h + j
-                    nc.scalar.activation(scaled[:, a, queries], scores[:], ACT.Copy, scale=ks_cols[:, a : a + 1])
+                scores = psum.tile([P, HALF], F32, tag=f"bank{2 * b + h}", name=f"scores{b}{h}")
+                nc.tensor.matmul_mx(
+                    out=scores[:],
+                    lhsT=q_mx[b][0][:].bitcast(FP8X4),
+                    lhsT_scale=q_mx[b][1][:],
+                    rhs=k_mx[h][0][:].bitcast(FP8X4),
+                    rhs_scale=k_mx[h][1][:],
+                    start=True,
+                    stop=True,
+                )
+                part = slice(h * S // 2, (h + 1) * S // 2)
+                nc.vector.tensor_tensor(scaled[b][:, :, part], scores[:].rearrange("p (s a) -> p a s", a=PACK), ks_row[:, :, part], ALU.mult)
 
-        v_words = []
-        for e in range(DV // P):
-            v_bf = keep.tile([P, N], BF16, name=f"v_bf{e}", tag=f"v_bf{e}", align_bytes=64)
-            if e == 0:
-                dealt = v_bf[:].rearrange("p (u s i) -> p s u i", u=2, i=2)
-                nc.vector.tensor_copy(dealt[:, : S // 2], v_raw[e][:, :HEAD].indirect(offsets[:, :16]))
-                nc.vector.tensor_copy(dealt[:, S // 2 :], v_raw[e][:].indirect(offsets[:, 16:]))
-            else:
-                nc.vector.tensor_copy(v_bf[:], v_raw[e][:].indirect(offsets[:]))
-            v_words.append(v_bf[:].bitcast(F32))
+        v_bf = [keep.tile([P, N], BF16, name=f"v_bf{e}", align_bytes=64) for e in range(2)]
+        nc.scalar.activation(v_bf[0][:], v_raw[0][:].indirect(offsets[:]), ACT.Copy)
         v_grouped = []
 
         def turn_values(e):
-            turned = psum.tile([P, 2, P], F32, tag=f"bank{3 + 2 * e}", name=f"v_turned{e}")
+            turned = psum.tile([P, 2, P], F32, tag=f"bank{4 + e}", name=f"v_turned{e}")
             for u in range(2):
-                nc.tensor.transpose(turned[:, u, :], v_words[e][:, u::2] if e == 1 else v_words[e][:, u * S : (u + 1) * S], ident[:])
-            if e == 0:
-                grouped = late.tile([P, P * PACK], BF16, name="v_grouped0", align_bytes=64, offset=0)
-            else:
-                grouped = keep.tile([P, P * PACK], BF16, name="v_grouped1", align_bytes=64)
+                nc.tensor.transpose(turned[:, u, :], v_bf[e][:].bitcast(F32)[:, u::2], ident[:])
+            grouped = keep.tile([P, P * PACK], BF16, name=f"v_grouped{e}", align_bytes=64)
             nc.scalar.copy(grouped[:].bitcast(F32).rearrange("p (f u) -> p f u", u=2), turned[:].rearrange("p u f -> p f u"))
             v_grouped.append(grouped)
 
-        neg_max = []
         parts = [keep.tile([P, 2], F32, name=f"parts{h}") for h in range(2)]
         probs = []
         for b in range(2):
-            rows = psum.tile([P, PACK, S], F32, tag=f"bank{4 + b}", name=f"rows{b}")
-            for a in range(PACK):
-                nc.tensor.transpose(rows[:, a, :], scaled[:, a, b * P : (b + 1) * P], ident[:])
-            if b == 0:
-                top = late.tile([P, 1], F32, name="top0", align_bytes=64, offset=0)
-            else:
-                top = late.tile([P, 1], F32, name="top1", align_bytes=64, offset=2048)
-            nc.vector.reduce_max(out=top[:], in_=rows[:].rearrange("p a s -> p (a s)"), axis=AX.X, negate=True)
-            neg_max.append(top)
-            prob = keep.tile([P, PACK, S], F32, name=f"prob{b}")
-            by_class = rows[:].rearrange("p n (s a) -> p a n s", a=PACK)
+            top = keep.tile([P, 1], F32, name=f"top{b}")
+            nc.vector.reduce_max(out=top[:], in_=scaled[b][:].rearrange("p a s -> p (a s)"), axis=AX.X, negate=True)
+            prob = late.tile([P, PACK, S], F32, name=f"prob{b}", align_bytes=64, offset=b * 4 * N)
             for h in range(2):
                 nc.scalar.activation(
-                    prob[:, 2 * h : 2 * h + 2, :].rearrange("p a (n s) -> p a n s", n=PACK),
-                    by_class[:, 2 * h : 2 * h + 2, :, :],
+                    prob[:, 2 * h : 2 * h + 2, :],
+                    scaled[b][:, 2 * h : 2 * h + 2, :],
                     ACT.Exp,
                     bias=top[:],
                     accum_out=parts[h][:, b : b + 1],
                 )
             probs.append(prob)
+            if b == 0:
+                turn_values(0)
 
-        turn_values(0)
+        nc.vector.tensor_copy(v_bf[1][:, :SHARE], v_raw[1][:].indirect(offsets[:, : SHARE // 16]))
+        nc.scalar.activation(v_bf[1][:, SHARE:], v_raw[1][:].indirect(offsets[:, SHARE // 16 :]), ACT.Copy)
+
         p_turned = []
         for b in range(2):
             turned = psum.tile([P, PACK, P], F32, tag=f"bank{6 + b}", name=f"p_turned{b}")
@@ -192,12 +169,10 @@ def tile_attend_gate_topks_kernel(tc, qT, kT, vT, ks, vs, og, offs, out):
 
         half = keep.tile([P, 2, DV], F32, name="half")
         nc.scalar.activation(half[:], og_raw[:], ACT.Tanh, scale=0.5)
-        gate = keep.tile([P, 2, DV], F32, name="gate", tag="v_bf1", align_bytes=64)
+        gate = keep.tile([P, 2, DV], F32, name="gate")
         for b in range(2):
-            nc.scalar.activation(gate[:, b, :], half[:, b, :], ACT.Identity, scale=0.5, bias=0.5)
+            nc.gpsimd.tensor_scalar(gate[:, b, :], half[:, b, :], 0.5, 0.5, ALU.mult, ALU.add)
 
-        v_codes = late.tile([P, DV], U32, name="v_codes", align_bytes=64, offset=4 * T + 2048)
-        v_scales = keep.tile([P, DV], U8, name="v_scales", align_bytes=64)
         def weigh(b, weights):
             nc.vector.tensor_tensor(
                 weights[:],
@@ -207,32 +182,28 @@ def tile_attend_gate_topks_kernel(tc, qT, kT, vT, ks, vs, og, offs, out):
             )
             return weights[:].rearrange("p q a -> p (q a)")
 
-        def quantise_values(e):
-            cols = slice(e * P, (e + 1) * P)
-            nc.vector.quantize_mx(out=v_codes[:, cols].bitcast(FP8X4), scales=v_scales[:, cols], in_=v_grouped[e][:])
-
         sums = keep.tile([P, 2], F32, name="sums")
         nc.gpsimd.tensor_tensor(sums[:], parts[0][:], parts[1][:], ALU.add)
-        w_first = weigh(0, late.tile([P, P, PACK], BF16, name="w_bf0", align_bytes=64, offset=2048))
+        w_first = weigh(0, late.tile([P, P, PACK], BF16, name="w_bf0", align_bytes=64, offset=4 * T))
+        v_mx = [quantise("v0", v_grouped[0][:], P, 4 * T + 2048)]
+        w_second = weigh(1, late.tile([P, P, PACK], BF16, name="w_bf1", align_bytes=64, offset=4 * T + 1024))
+        w_mx = [quantise("w0", w_first, P)]
         inv = late.tile([P, 2], F32, name="inv", align_bytes=64, offset=4 * T + 3072)
         nc.vector.reciprocal(inv[:], sums[:])
-        quantise_values(0)
-        w_second = weigh(1, late.tile([P, P, PACK], BF16, name="w_bf1", align_bytes=64, offset=4 * T))
-        w_mx = [quantise("w0", w_first, P, "w0"), quantise("w1", w_second, P, "w1")]
-        quantise_values(1)
+        w_mx.append(quantise("w1", w_second, P))
+        v_mx.append(quantise("v1", v_grouped[1][:], P))
 
         result = [keep.tile([P, DV], F32, name=f"result{b}") for b in range(2)]
         for e in range(2):
             cols = slice(e * P, (e + 1) * P)
             for b in range(2):
-                w_codes, w_scales = w_mx[b]
                 y = psum.tile([P, P], F32, tag=f"bank{2 * e + b}", name=f"y{b}{e}")
                 nc.tensor.matmul_mx(
                     out=y[:],
-                    lhsT=w_codes[:].bitcast(FP8X4),
-                    lhsT_scale=w_scales[:],
-                    rhs=v_codes[:, cols].bitcast(FP8X4),
-                    rhs_scale=v_scales[:, cols],
+                    lhsT=w_mx[b][0][:].bitcast(FP8X4),
+                    lhsT_scale=w_mx[b][1][:],
+                    rhs=v_mx[e][0][:].bitcast(FP8X4),
+                    rhs_scale=v_mx[e][1][:],
                     start=True,
                     stop=True,
                 )

@@ -10,7 +10,7 @@ S = N // PACK
 HALF = N // 2
 HEAD = T - HALF
 ROW = P - 1
-SHARE = 3 * N // 4
+LEAD = T // 4
 
 FLOPS = 2 * NQ * N * D + 2 * NQ * N * DV
 BYTES = 4 * (D * NQ + D * T + DV * T + 2 * T + 2 * NQ * DV) + 2 * P * (N // 16)
@@ -41,10 +41,11 @@ def tile_attend_gate_topks_kernel(tc, qT, kT, vT, ks, vs, og, offs, out):
 
         k_rows = kT.rearrange("(p t) n -> p t n", t=PACK)
         k_raw = [keep.tile([P, T], F32, name=f"k_raw{t}") for t in range(PACK)]
-        nc.sync.dma_start(out=k_raw[0][:], in_=k_rows[:, 0, :])
+        nc.sync.dma_start(out=k_raw[0][:, :LEAD], in_=k_rows[:, 0, :LEAD])
         nc.sync.dma_start(offsets[:], offs)
         nc.sync.dma_start(out=scale_win[0][ROW:, :], in_=ks[0:1, :])
         nc.sync.dma_start(out=scale_win[1][ROW:, :], in_=vs[0:1, :])
+        nc.sync.dma_start(out=k_raw[0][:, LEAD:], in_=k_rows[:, 0, LEAD:])
         nc.sync.dma_start(out=k_raw[1][:], in_=k_rows[:, 1, :])
         nc.sync.dma_start(out=k_raw[2][:], in_=k_rows[:, 2, :])
         nc.sync.dma_start(out=k_raw[3][:, :HEAD], in_=k_rows[:, 3, :HEAD])
@@ -156,8 +157,7 @@ def tile_attend_gate_topks_kernel(tc, qT, kT, vT, ks, vs, og, offs, out):
             if b == 0:
                 turn_values(0)
 
-        nc.vector.tensor_copy(v_bf[1][:, :SHARE], v_raw[1][:].indirect(offsets[:, : SHARE // 16]))
-        nc.scalar.activation(v_bf[1][:, SHARE:], v_raw[1][:].indirect(offsets[:, SHARE // 16 :]), ACT.Copy)
+        nc.vector.tensor_copy(v_bf[1][:], v_raw[1][:].indirect(offsets[:]))
 
         p_turned = []
         for b in range(2):
@@ -171,7 +171,7 @@ def tile_attend_gate_topks_kernel(tc, qT, kT, vT, ks, vs, og, offs, out):
         nc.scalar.activation(half[:], og_raw[:], ACT.Tanh, scale=0.5)
         gate = keep.tile([P, 2, DV], F32, name="gate")
         for b in range(2):
-            nc.gpsimd.tensor_scalar(gate[:, b, :], half[:, b, :], 0.5, 0.5, ALU.mult, ALU.add)
+            nc.scalar.activation(gate[:, b, :], half[:, b, :], ACT.Identity, scale=0.5, bias=0.5)
 
         def weigh(b, weights):
             nc.vector.tensor_tensor(

@@ -111,7 +111,7 @@ def tile_attend_gate_topks_kernel(tc, qT, kT, vT, ks, vs, og, offs, out):
             k_mx.append(quantise(f"k{i}", k_bf[i][:].rearrange("p s t -> p (s t)"), HALF))
             q_mx.append(quantise(f"q{i}", q_bf[i][:].rearrange("p q t -> p (q t)"), P))
 
-        scaled = [keep.tile([P, PACK, S], F32, name=f"scaled{b}") for b in range(2)]
+        scaled = [keep.tile([P, PACK, S], F32, name=f"scaled{b}", tag=f"scaled{b}", align_bytes=64) for b in range(2)]
         for b in range(2):
             for h in range(2):
                 scores = psum.tile([P, HALF], F32, tag=f"bank{2 * b + h}", name=f"scores{b}{h}")
@@ -135,7 +135,7 @@ def tile_attend_gate_topks_kernel(tc, qT, kT, vT, ks, vs, og, offs, out):
             turned = psum.tile([P, 2, P], F32, tag=f"bank{4 + e}", name=f"v_turned{e}")
             for u in range(2):
                 nc.tensor.transpose(turned[:, u, :], v_bf[e][:].bitcast(F32)[:, u::2], ident[:])
-            grouped = keep.tile([P, P * PACK], BF16, name=f"v_grouped{e}", align_bytes=64)
+            grouped = keep.tile([P, P * PACK], BF16, name=f"v_grouped{e}", tag=("scaled1", "v_grouped1")[e], align_bytes=64)
             nc.scalar.copy(grouped[:].bitcast(F32).rearrange("p (f u) -> p f u", u=2), turned[:].rearrange("p u f -> p f u"))
             v_grouped.append(grouped)
 
@@ -144,7 +144,7 @@ def tile_attend_gate_topks_kernel(tc, qT, kT, vT, ks, vs, og, offs, out):
         for b in range(2):
             top = keep.tile([P, 1], F32, name=f"top{b}")
             nc.vector.reduce_max(out=top[:], in_=scaled[b][:].rearrange("p a s -> p (a s)"), axis=AX.X, negate=True)
-            prob = late.tile([P, PACK, S], F32, name=f"prob{b}", align_bytes=64, offset=b * 4 * N)
+            prob = keep.tile([P, PACK, S], F32, name=f"prob{b}", align_bytes=64)
             for h in range(2):
                 nc.scalar.activation(
                     prob[:, 2 * h : 2 * h + 2, :],
@@ -154,10 +154,9 @@ def tile_attend_gate_topks_kernel(tc, qT, kT, vT, ks, vs, og, offs, out):
                     accum_out=parts[h][:, b : b + 1],
                 )
             probs.append(prob)
-            if b == 0:
-                turn_values(0)
 
         nc.vector.tensor_copy(v_bf[1][:], v_raw[1][:].indirect(offsets[:]))
+        turn_values(0)
 
         p_turned = []
         for b in range(2):

@@ -55,7 +55,11 @@ def tile_attend_gate_topks_kernel(tc, qT, kT, vT, ks, vs, og, offs, out):
         v_raw = []
         for e in range(DV // P):
             block = late.tile([P, T], F32, name=f"v_raw{e}", align_bytes=64, offset=e * 4 * T)
-            nc.sync.dma_start(out=block[:], in_=vT[e * P : (e + 1) * P, :])
+            if e == 0:
+                nc.sync.dma_start(out=block[:], in_=vT[:P, :])
+            else:
+                nc.sync.dma_start(out=block[:, :HEAD], in_=vT[P:, :HEAD])
+                nc.sync.dma_start(out=block[:, HEAD:], in_=vT[P:, HEAD:])
             v_raw.append(block)
         og_raw = keep.tile([P, 2, DV], F32, name="og_raw")
         nc.sync.dma_start(out=og_raw[:], in_=og.rearrange("o (b p) e -> p (o b) e", p=P))
@@ -134,7 +138,8 @@ def tile_attend_gate_topks_kernel(tc, qT, kT, vT, ks, vs, og, offs, out):
         def turn_values(e):
             turned = psum.tile([P, 2, P], F32, tag=f"bank{4 + e}", name=f"v_turned{e}")
             for u in range(2):
-                nc.tensor.transpose(turned[:, u, :], v_bf[e][:].bitcast(F32)[:, u::2], ident[:])
+                words = v_bf[e][:].bitcast(F32)
+                nc.tensor.transpose(turned[:, u, :], words[:, u::2] if e == 0 else words[:, u * S : (u + 1) * S], ident[:])
             grouped = keep.tile([P, P * PACK], BF16, name=f"v_grouped{e}", tag=("scaled1", "v_grouped1")[e], align_bytes=64)
             nc.scalar.copy(grouped[:].bitcast(F32).rearrange("p (f u) -> p f u", u=2), turned[:].rearrange("p u f -> p f u"))
             v_grouped.append(grouped)
@@ -155,7 +160,9 @@ def tile_attend_gate_topks_kernel(tc, qT, kT, vT, ks, vs, og, offs, out):
                 )
             probs.append(prob)
 
-        nc.vector.tensor_copy(v_bf[1][:], v_raw[1][:].indirect(offsets[:]))
+        dealt = v_bf[1][:].rearrange("p (u s i) -> p s u i", u=2, i=2)
+        nc.vector.tensor_copy(dealt[:, : S // 2], v_raw[1][:, :HEAD].indirect(offsets[:, :16]))
+        nc.vector.tensor_copy(dealt[:, S // 2 :], v_raw[1][:].indirect(offsets[:, 16:]))
         turn_values(0)
 
         p_turned = []

@@ -191,18 +191,18 @@ def tile_attend_gate_topks_kernel(tc, qT, kT, vT, ks, vs, og, offs, out):
         sums = keep.tile([P, 2], F32, name="sums")
         nc.gpsimd.tensor_tensor(sums[:], parts[0][:], parts[1][:], ALU.add)
         w_first = weigh(0, late.tile([P, P, PACK], BF16, name="w_bf0", align_bytes=64, offset=4 * T))
-        v_mx = [quantise("v0", v_grouped[0][:], P, 4 * T + 2048)]
-        w_second = weigh(1, late.tile([P, P, PACK], BF16, name="w_bf1", align_bytes=64, offset=4 * T + 1024))
-        w_mx = [quantise("w0", w_first, P)]
         inv = late.tile([P, 2], F32, name="inv", align_bytes=64, offset=4 * T + 3072)
         nc.vector.reciprocal(inv[:], sums[:])
-        w_mx.append(quantise("w1", w_second, P))
+        w_mx = [quantise("w0", w_first, P)]
+        v_mx = [quantise("v0", v_grouped[0][:], P, 4 * T + 2048)]
+        w_second = weigh(1, late.tile([P, P, PACK], BF16, name="w_bf1", align_bytes=64, offset=4 * T + 1024))
         v_mx.append(quantise("v1", v_grouped[1][:], P))
+        w_mx.append(quantise("w1", w_second, P))
 
         result = [keep.tile([P, DV], F32, name=f"result{b}") for b in range(2)]
-        for e in range(2):
-            cols = slice(e * P, (e + 1) * P)
-            for b in range(2):
+        for b in range(2):
+            for e in range(2):
+                cols = slice(e * P, (e + 1) * P)
                 y = psum.tile([P, P], F32, tag=f"bank{2 * e + b}", name=f"y{b}{e}")
                 nc.tensor.matmul_mx(
                     out=y[:],

@@ -35,12 +35,12 @@ def tile_attend_gate_topks_kernel(tc, qT, kT, vT, ks, vs, og, offs, out):
         psum = ctx.enter_context(tc.psum_pool(name="psum", bufs=1))
 
         offsets = keep.tile([P, N // 16], U16, name="offsets")
-        scale_win = [keep.tile([P, T], F32, name=f"scale_win{i}") for i in range(2)]
+        scale_win = [keep.tile([P, T], F32, name=f"scale_win{i}", align_bytes=256) for i in range(2)]
         for win in scale_win:
             nc.vector.memset(win[:ROW, :], 0.0)
 
         k_rows = kT.rearrange("(p t) n -> p t n", t=PACK)
-        k_raw = [keep.tile([P, T], F32, name=f"k_raw{t}") for t in range(PACK)]
+        k_raw = [keep.tile([P, T], F32, name=f"k_raw{t}", align_bytes=256) for t in range(PACK)]
         nc.sync.dma_start(out=k_raw[0][:, :LEAD], in_=k_rows[:, 0, :LEAD])
         nc.sync.dma_start(offsets[:], offs)
         nc.sync.dma_start(out=scale_win[0][ROW:, :], in_=ks[0:1, :])
@@ -49,19 +49,19 @@ def tile_attend_gate_topks_kernel(tc, qT, kT, vT, ks, vs, og, offs, out):
         nc.sync.dma_start(out=k_raw[1][:], in_=k_rows[:, 1, :])
         nc.sync.dma_start(out=k_raw[2][:], in_=k_rows[:, 2, :])
         nc.sync.dma_start(out=k_raw[3][:, :HEAD], in_=k_rows[:, 3, :HEAD])
-        q_raw = keep.tile([P, PACK, NQ], F32, name="q_raw")
+        q_raw = keep.tile([P, PACK, NQ], F32, name="q_raw", align_bytes=256)
         nc.sync.dma_start(out=q_raw[:], in_=qT.rearrange("o (p t) q -> p (o t) q", t=PACK))
         nc.sync.dma_start(out=k_raw[3][:, HEAD:], in_=k_rows[:, 3, HEAD:])
         v_raw = []
         for e in range(DV // P):
-            block = late.tile([P, T], F32, name=f"v_raw{e}", align_bytes=64, offset=e * 4 * T)
+            block = late.tile([P, T], F32, name=f"v_raw{e}", align_bytes=256, offset=e * 4 * T)
             if e == 0:
                 nc.sync.dma_start(out=block[:], in_=vT[:P, :])
             else:
                 nc.sync.dma_start(out=block[:, :HEAD], in_=vT[P:, :HEAD])
                 nc.sync.dma_start(out=block[:, HEAD:], in_=vT[P:, HEAD:])
             v_raw.append(block)
-        og_raw = keep.tile([P, 2, DV], F32, name="og_raw")
+        og_raw = keep.tile([P, 2, DV], F32, name="og_raw", align_bytes=256)
         nc.sync.dma_start(out=og_raw[:], in_=og.rearrange("o (b p) e -> p (o b) e", p=P))
 
         ident = keep.tile([P, P], F32, name="ident")
@@ -199,7 +199,7 @@ def tile_attend_gate_topks_kernel(tc, qT, kT, vT, ks, vs, og, offs, out):
         v_mx.append(quantise("v1", v_grouped[1][:], P))
         w_mx.append(quantise("w1", w_second, P))
 
-        result = [keep.tile([P, DV], F32, name=f"result{b}") for b in range(2)]
+        result = [keep.tile([P, DV], F32, name=f"result{b}", align_bytes=256) for b in range(2)]
         for b in range(2):
             for e in range(2):
                 cols = slice(e * P, (e + 1) * P)

@@ -9,7 +9,7 @@ PACK = 4
 S = N // PACK
 HALF = N // 2
 HEAD = T - HALF
-ROW = P - 1
+ROWS = (P - 1, P // 2 - 1)
 LEAD = T // 4
 
 FLOPS = 2 * NQ * N * D + 2 * NQ * N * DV
@@ -36,15 +36,16 @@ def tile_attend_gate_topks_kernel(tc, qT, kT, vT, ks, vs, og, offs, out):
 
         offsets = keep.tile([P, N // 16], U16, name="offsets")
         scale_win = [keep.tile([P, T], F32, name=f"scale_win{i}", align_bytes=256) for i in range(2)]
-        for win in scale_win:
-            nc.vector.memset(win[:ROW, :], 0.0)
+        for i, win in enumerate(scale_win):
+            nc.vector.memset(win[: ROWS[i], :], 0.0)
+        nc.vector.memset(scale_win[1][ROWS[1] + 1 :, :], 0.0)
 
         k_rows = kT.rearrange("(p t) n -> p t n", t=PACK)
         k_raw = [keep.tile([P, T], F32, name=f"k_raw{t}", align_bytes=256) for t in range(PACK)]
         nc.sync.dma_start(out=k_raw[0][:, :LEAD], in_=k_rows[:, 0, :LEAD])
         nc.sync.dma_start(offsets[:], offs)
-        nc.sync.dma_start(out=scale_win[0][ROW:, :], in_=ks[0:1, :])
-        nc.sync.dma_start(out=scale_win[1][ROW:, :], in_=vs[0:1, :])
+        nc.sync.dma_start(out=scale_win[0][ROWS[0] : ROWS[0] + 1, :], in_=ks[0:1, :])
+        nc.sync.dma_start(out=scale_win[1][ROWS[1] : ROWS[1] + 1, :], in_=vs[0:1, :])
         nc.sync.dma_start(out=k_raw[0][:, LEAD:], in_=k_rows[:, 0, LEAD:])
         nc.sync.dma_start(out=k_raw[1][:], in_=k_rows[:, 1, :])
         nc.sync.dma_start(out=k_raw[2][:], in_=k_rows[:, 2, :])
@@ -83,7 +84,7 @@ def tile_attend_gate_topks_kernel(tc, qT, kT, vT, ks, vs, og, offs, out):
             for a in range(PACK):
                 nc.tensor.transpose(turned[:, a, :], picked[:, a::PACK], ident[:])
             cols = keep.tile([P, PACK], F32, name=f"scale_cols{i}")
-            nc.scalar.copy(cols[:], turned[:, :, ROW])
+            nc.scalar.copy(cols[:], turned[:, :, ROWS[i]])
             scale_cols.append(cols)
         ks_cols, vs_cols = scale_cols
         spread = psum.tile([P, PACK, S], F32, tag="bank2", name="ks_spread")

from contextlib import ExitStack

import concourse.mybir as mybir
from concourse.masks import make_identity

P = 128
D, NQ, T, N, DV = 512, 256, 2048, 512, 256
PACK = 4
S = N // PACK
HALF = N // 2
HEAD = T - HALF
ROWS = (P - 1, P // 2 - 1)
LEAD = T // 4

FLOPS = 2 * NQ * N * D + 2 * NQ * N * DV
BYTES = 4 * (D * NQ + D * T + DV * T + 2 * T + 2 * NQ * DV) + 2 * P * (N // 16)

F32 = mybir.dt.float32
BF16 = mybir.dt.bfloat16
U16 = mybir.dt.uint16
U32 = mybir.dt.uint32
U8 = mybir.dt.uint8
FP8X4 = mybir.dt.float8_e4m3fn_x4

ACT = mybir.ActivationFunctionType
ALU = mybir.AluOpType
AX = mybir.AxisListType


def tile_attend_gate_topks_kernel(tc, qT, kT, vT, ks, vs, og, offs, out):
    nc = tc.nc
    with ExitStack() as ctx:
        keep = ctx.enter_context(tc.tile_pool(name="keep", bufs=1))
        late = ctx.enter_context(tc.tile_pool(name="late", bufs=1))
        psum = ctx.enter_context(tc.psum_pool(name="psum", bufs=1))

        offsets = keep.tile([P, N // 16], U16, name="offsets")
        scale_win = [keep.tile([P, T], F32, name=f"scale_win{i}", align_bytes=256) for i in range(2)]
        for i, win in enumerate(scale_win):
            nc.vector.memset(win[: ROWS[i], :], 0.0)
        nc.vector.memset(scale_win[1][ROWS[1] + 1 :, :], 0.0)

        k_rows = kT.rearrange("(p t) n -> p t n", t=PACK)
        k_raw = [keep.tile([P, T], F32, name=f"k_raw{t}", align_bytes=256) for t in range(PACK)]
        nc.sync.dma_start(out=k_raw[0][:, :LEAD], in_=k_rows[:, 0, :LEAD])
        nc.sync.dma_start(offsets[:], offs)
        nc.sync.dma_start(out=scale_win[0][ROWS[0] : ROWS[0] + 1, :], in_=ks[0:1, :])
        nc.sync.dma_start(out=scale_win[1][ROWS[1] : ROWS[1] + 1, :], in_=vs[0:1, :])
        nc.sync.dma_start(out=k_raw[0][:, LEAD:], in_=k_rows[:, 0, LEAD:])
        nc.sync.dma_start(out=k_raw[1][:], in_=k_rows[:, 1, :])
        nc.sync.dma_start(out=k_raw[2][:], in_=k_rows[:, 2, :])
        nc.sync.dma_start(out=k_raw[3][:, :HEAD], in_=k_rows[:, 3, :HEAD])
        q_raw = keep.tile([P, PACK, NQ], F32, name="q_raw", align_bytes=256)
        nc.sync.dma_start(out=q_raw[:], in_=qT.rearrange("o (p t) q -> p (o t) q", t=PACK))
        nc.sync.dma_start(out=k_raw[3][:, HEAD:], in_=k_rows[:, 3, HEAD:])
        v_raw = []
        for e in range(DV // P):
            block = late.tile([P, T], F32, name=f"v_raw{e}", align_bytes=256, offset=e * 4 * T)
            if e == 0:
                nc.sync.dma_start(out=block[:], in_=vT[:P, :])
            else:
                nc.sync.dma_start(out=block[:, :HEAD], in_=vT[P:, :HEAD])
                nc.sync.dma_start(out=block[:, HEAD:], in_=vT[P:, HEAD:])
            v_raw.append(block)
        og_raw = keep.tile([P, 2, DV], F32, name="og_raw", align_bytes=256)
        nc.sync.dma_start(out=og_raw[:], in_=og.rearrange("o (b p) e -> p (o b) e", p=P))

        ident = keep.tile([P, P], F32, name="ident")
        make_identity(nc, ident[:])

        k_bf = [keep.tile([P, HALF, PACK], BF16, name=f"k_half{h}", align_bytes=64) for h in range(2)]
        for t in range(PACK):
            for h in range(2):
                nc.vector.tensor_copy(k_bf[h][:, :, t], k_raw[t][:, : HEAD if h == 0 else T].indirect(offsets[:, h * 16 : (h + 1) * 16]))

        scale_cols = []
        for i in range(2):
            picked = keep.tile([P, N], F32, name=f"scale_row{i}", tag="scale_row")
            if i == 0:
                nc.vector.tensor_copy(picked[:], scale_win[i][:].indirect(offsets[:]))
            else:
                nc.scalar.activation(picked[:], scale_win[i][:].indirect(offsets[:]), ACT.Copy)
            turned = psum.tile([P, PACK, P], F32, tag=f"bank{i}", name=f"scale_turned{i}")
            for a in range(PACK):
                nc.tensor.transpose(turned[:, a, :], picked[:, a::PACK], ident[:])
            cols = keep.tile([P, PACK], F32, name=f"scale_cols{i}")
            nc.scalar.copy(cols[:], turned[:, :, ROWS[i]])
            scale_cols.append(cols)
        ks_cols, vs_cols = scale_cols
        spread = psum.tile([P, PACK, S], F32, tag="bank2", name="ks_spread")
        for a in range(PACK):
            nc.tensor.transpose(spread[:, a, :], ks_cols[:, a : a + 1].to_broadcast([P, P]), ident[:])
        ks_row = keep.tile([P, PACK, S], F32, name="ks_row")
        nc.scalar.copy(ks_row[:], spread[:])

        q_bf = []
        for b in range(2):
            grouped = keep.tile([P, P, PACK], BF16, name=f"q_bf{b}", align_bytes=64)
            nc.scalar.copy(
                grouped[:].rearrange("p (c i) t -> p c t i", i=PACK),
                q_raw[:, :, b * P : (b + 1) * P].rearrange("p t (c i) -> p c t i", i=PACK),
            )
            q_bf.append(grouped)

        def quantise(name, source, width, offset=None):
            if offset is None:
                codes = keep.tile([P, width], U32, name=f"{name}_codes", align_bytes=64)
            else:
                codes = late.tile([P, width], U32, name=f"{name}_codes", align_bytes=64, offset=offset)
            scales = keep.tile([P, width], U8, name=f"{name}_scales", align_bytes=64)
            nc.vector.quantize_mx(out=codes[:].bitcast(FP8X4), scales=scales[:], in_=source)
            return codes, scales

        k_mx, q_mx = [], []
        for i in range(2):
            k_mx.append(quantise(f"k{i}", k_bf[i][:].rearrange("p s t -> p (s t)"), HALF))
            q_mx.append(quantise(f"q{i}", q_bf[i][:].rearrange("p q t -> p (q t)"), P))

        scaled = [keep.tile([P, PACK, S], F32, name=f"scaled{b}", tag=f"scaled{b}", align_bytes=64) for b in range(2)]
        for b in range(2):
            for h in range(2):
                scores = psum.tile([P, HALF], F32, tag=f"bank{2 * b + h}", name=f"scores{b}{h}")
                nc.tensor.matmul_mx(
                    out=scores[:],
                    lhsT=q_mx[b][0][:].bitcast(FP8X4),
                    lhsT_scale=q_mx[b][1][:],
                    rhs=k_mx[h][0][:].bitcast(FP8X4),
                    rhs_scale=k_mx[h][1][:],
                    start=True,
                    stop=True,
                )
                part = slice(h * S // 2, (h + 1) * S // 2)
                nc.vector.tensor_tensor(scaled[b][:, :, part], scores[:].rearrange("p (s a) -> p a s", a=PACK), ks_row[:, :, part], ALU.mult)

        v_bf = [keep.tile([P, N], BF16, name=f"v_bf{e}", align_bytes=64) for e in range(2)]
        nc.scalar.activation(v_bf[0][:], v_raw[0][:].indirect(offsets[:]), ACT.Copy)
        v_grouped = []

        def turn_values(e):
            turned = psum.tile([P, 2, P], F32, tag=f"bank{4 + e}", name=f"v_turned{e}")
            for u in range(2):
                words = v_bf[e][:].bitcast(F32)
                nc.tensor.transpose(turned[:, u, :], words[:, u::2] if e == 0 else words[:, u * S : (u + 1) * S], ident[:])
            grouped = keep.tile([P, P * PACK], BF16, name=f"v_grouped{e}", tag=("scaled1", "v_grouped1")[e], align_bytes=64)
            nc.scalar.copy(grouped[:].bitcast(F32).rearrange("p (f u) -> p f u", u=2), turned[:].rearrange("p u f -> p f u"))
            v_grouped.append(grouped)

        parts = [keep.tile([P, 2], F32, name=f"parts{h}") for h in range(2)]
        probs = []
        for b in range(2):
            top = keep.tile([P, 1], F32, name=f"top{b}")
            nc.vector.reduce_max(out=top[:], in_=scaled[b][:].rearrange("p a s -> p (a s)"), axis=AX.X, negate=True)
            prob = keep.tile([P, PACK, S], F32, name=f"prob{b}", align_bytes=64)
            for h in range(2):
                nc.scalar.activation(
                    prob[:, 2 * h : 2 * h + 2, :],
                    scaled[b][:, 2 * h : 2 * h + 2, :],
                    ACT.Exp,
                    bias=top[:],
                    accum_out=parts[h][:, b : b + 1],
                )
            probs.append(prob)

        dealt = v_bf[1][:].rearrange("p (u s i) -> p s u i", u=2, i=2)
        nc.vector.tensor_copy(dealt[:, : S // 2], v_raw[1][:, :HEAD].indirect(offsets[:, :16]))
        nc.vector.tensor_copy(dealt[:, S // 2 :], v_raw[1][:].indirect(offsets[:, 16:]))
        turn_values(0)

        p_turned = []
        for b in range(2):
            turned = psum.tile([P, PACK, P], F32, tag=f"bank{6 + b}", name=f"p_turned{b}")
            for a in range(PACK):
                nc.tensor.transpose(turned[:, a, :], probs[b][:, a, :], ident[:])
            p_turned.append(turned)
        turn_values(1)

        half = keep.tile([P, 2, DV], F32, name="half")
        nc.scalar.activation(half[:], og_raw[:], ACT.Tanh, scale=0.5)
        gate = keep.tile([P, 2, DV], F32, name="gate")
        for b in range(2):
            nc.scalar.activation(gate[:, b, :], half[:, b, :], ACT.Identity, scale=0.5, bias=0.5)

        def weigh(b, weights):
            nc.vector.tensor_tensor(
                weights[:],
                p_turned[b][:].rearrange("p a q -> p q a"),
                vs_cols[:].unsqueeze(1).to_broadcast([P, P, PACK]),
                ALU.mult,
            )
            return weights[:].rearrange("p q a -> p (q a)")

        sums = keep.tile([P, 2], F32, name="sums")
        nc.gpsimd.tensor_tensor(sums[:], parts[0][:], parts[1][:], ALU.add)
        w_first = weigh(0, late.tile([P, P, PACK], BF16, name="w_bf0", align_bytes=64, offset=4 * T))
        inv = late.tile([P, 2], F32, name="inv", align_bytes=64, offset=4 * T + 3072)
        nc.vector.reciprocal(inv[:], sums[:])
        w_mx = [quantise("w0", w_first, P)]
        v_mx = [quantise("v0", v_grouped[0][:], P, 4 * T + 2048)]
        w_second = weigh(1, late.tile([P, P, PACK], BF16, name="w_bf1", align_bytes=64, offset=4 * T + 1024))
        v_mx.append(quantise("v1", v_grouped[1][:], P))
        w_mx.append(quantise("w1", w_second, P))

        result = [keep.tile([P, DV], F32, name=f"result{b}", align_bytes=256) for b in range(2)]
        for b in range(2):
            for e in range(2):
                cols = slice(e * P, (e + 1) * P)
                y = psum.tile([P, P], F32, tag=f"bank{2 * e + b}", name=f"y{b}{e}")
                nc.tensor.matmul_mx(
                    out=y[:],
                    lhsT=w_mx[b][0][:].bitcast(FP8X4),
                    lhsT_scale=w_mx[b][1][:],
                    rhs=v_mx[e][0][:].bitcast(FP8X4),
                    rhs_scale=v_mx[e][1][:],
                    start=True,
                    stop=True,
                )
                nc.vector.scalar_tensor_tensor(result[b][:, cols], y[:], inv[:, b : b + 1], gate[:, b, cols], ALU.mult, ALU.mult)
                if e == 1:
                    nc.sync.dma_start(out=out[0, b * P : (b + 1) * P, :], in_=result[b][:])
